import numpy as np
import ml_dtypes


def mxq(x, axis, fmt="e4m3"):
    dtype, down = {"e4m3": (ml_dtypes.float8_e4m3fn, 7), "e5m2": (ml_dtypes.float8_e5m2, 14)}[fmt]
    v = np.moveaxis(np.asarray(x, np.float32).astype(ml_dtypes.bfloat16).astype(np.float64), axis, -1)
    blocks = v.reshape(v.shape[:-1] + (-1, 32))
    amax = np.abs(blocks).max(-1, keepdims=True)
    byte = np.maximum(np.where(amax > 0, np.frexp(amax)[1] - 1 + 127, 0) - down, 1)
    scale = np.exp2(byte - 127.0)
    codes = (blocks / scale).astype(np.float32).astype(dtype).astype(np.float64)
    return np.moveaxis((codes * scale).reshape(v.shape), -1, axis)


WIDE = False


def mx_kscale(k):
    if not WIDE:
        return np.ones(k)
    levels = np.array([10, -10, 5, -5, 0])
    if k % 512:
        return np.exp2(np.random.permutation(np.resize(levels, k // 32))).repeat(32)
    a = np.empty((k // 512, 16))
    for p in range(k // 512):
        a[p, :8] = np.random.permutation(np.resize(levels, 8))
        for g in range(8):
            far = levels[np.abs(levels - a[p, g]) >= 10]
            a[p, g + 8] = far[np.random.randint(len(far))]
    return np.exp2(a.ravel()).repeat(32)


def f64(x):
    return np.asarray(x).astype(np.float64)


def striped(idx):
    return np.tile(idx.reshape(-1, 16).T, (8, 1)).astype(np.uint16)


def unstriped(offs):
    return offs[:16].T.reshape(-1).astype(np.int64)


def pack_weight(w):
    k, n = w.shape
    w = f64(np.asarray(w, np.float32).astype(ml_dtypes.bfloat16)).reshape(k // 32, 32, n)
    amax = np.abs(w).max(1)
    byte = np.clip(np.where(amax > 0, np.frexp(amax)[1] - 1 + 127 - 7, 1), 1, 254)
    scaled = (w * np.exp2(127.0 - byte)[:, None, :]).reshape(k, n).astype(np.float32)
    words = np.ascontiguousarray(scaled.reshape(k // 512, 128, 4, n).transpose(0, 1, 3, 2)).astype(ml_dtypes.float8_e4m3fn).view(np.uint8)
    return words, np.ascontiguousarray(byte.astype(np.uint8).reshape(k // 512, 16, n))


def unpack_weight(words, scales):
    g, p, n, _ = words.shape
    vals = np.ascontiguousarray(words).view(ml_dtypes.float8_e4m3fn).astype(np.float64) * np.repeat(np.exp2(scales.astype(np.float64) - 127.0), 8, axis=1)[..., None]
    return vals.transpose(0, 1, 3, 2).reshape(g * 512, n)


E2M1 = np.array([0.0, 0.5, 1.0, 1.5, 2.0, 3.0, 4.0, 6.0, -0.0, -0.5, -1.0, -1.5, -2.0, -3.0, -4.0, -6.0])


def pack_fp4(w):
    k, n = w.shape
    w = f64(np.asarray(w, np.float32).astype(ml_dtypes.bfloat16)).reshape(k // 32, 32, n)
    amax = np.abs(w).max(1)
    mant, ex = np.frexp(amax / 6.0)
    byte = np.clip(np.where(amax > 0, np.where(mant > 0.5, ex, ex - 1) + 127, 1), 1, 254)
    scaled = (w * np.exp2(127.0 - byte)[:, None, :]).reshape(k, n).astype(np.float32)
    c = np.ascontiguousarray(scaled.reshape(k // 512, 128, 4, n).transpose(0, 1, 3, 2)).astype(ml_dtypes.float4_e2m1fn).view(np.uint8) & 0xF
    words = (c[..., 0::2] | (c[..., 1::2] << 4)).reshape(k // 512, 128, 2 * n)
    return np.ascontiguousarray(words), np.ascontiguousarray(byte.astype(np.uint8).reshape(k // 512, 16, n))


def unpack_fp4(words, scales):
    g, _, n = scales.shape
    words = np.ascontiguousarray(words).reshape(g, 128, n, 2)
    nib = np.empty((g, 128, n, 4), np.uint8)
    nib[..., 0::2] = words & 0xF
    nib[..., 1::2] = words >> 4
    vals = E2M1[nib] * np.repeat(np.exp2(scales.astype(np.float64) - 127.0), 8, axis=1)[..., None]
    return vals.transpose(0, 1, 3, 2).reshape(g * 512, n)


def relu(v):
    return np.maximum(v, 0.0)

def planes(y):
    n, m = y.shape
    v = y.astype(np.float32).astype(ml_dtypes.bfloat16).astype(np.float64).reshape(n // 32, 32, m)
    top = np.abs(v).max(1)
    byte = np.clip(np.where(top > 0, np.frexp(top)[1] - 1 + 127 - 7, 1), 1, 254)
    codes = (v * np.exp2(127.0 - byte)[:, None, :]).reshape(n, m).astype(np.float32).astype(ml_dtypes.float8_e4m3fn).view(np.uint8)
    words = codes.reshape(n // 512, 128, 4, m).transpose(0, 1, 3, 2)
    return np.ascontiguousarray(words), np.ascontiguousarray(byte.astype(np.uint8).reshape(n // 512, 16, m))


K, T, S, D, V, H, U = 512, 2048, 512, 3, 512, 512, 1024
P = 2 ** 7


def setup_inputs():
    n = np.random.standard_normal
    s = mx_kscale(K)[:, None]
    u = mx_kscale(H)
    packed_xT = pack_weight(n((K, T)) * s)
    packed_w2 = pack_fp4(n((H, H)) / np.sqrt(H) / u[:, None])
    return {
        "x_words": packed_xT[0],
        "x_scales": packed_xT[1],
        "w1": (n((K, H)) / np.sqrt(K) / s * u).astype(np.float32),
        "w2_words": packed_w2[0],
        "w2_scales": packed_w2[1],
        "gate": np.tile(np.random.uniform(0.2, 0.6, (D, 1, V)), (1, P, 1)).astype(np.float32),
        "emb": (0.5 * n((H, U)) * u[:, None]).astype(np.float32),
        "offs": striped(np.random.permutation(T)[:S]),
        "cell": striped(np.random.permutation(U)[:S]),
        "pos1": striped(np.random.permutation(U)[:V]),
        "pos2": striped(np.random.permutation(U)[:V]),
        "pos3": striped(np.random.permutation(U)[:V]),
    }


def reference(x_words, x_scales, w1, w2_words, w2_scales, gate, emb, offs, cell, pos1, pos2, pos3):
    xq = unpack_weight(x_words, x_scales)[:, unstriped(offs)]
    up = np.zeros((H, U))
    up[:, unstriped(cell)] = relu(mxq(f64(w1), 0, "e4m3").T @ xq)
    z = up + f64(emb)
    y = unpack_fp4(w2_words, w2_scales).T @ mxq(z, 0, "e4m3")
    out_0 = y[:, unstriped(pos1)] * f64(gate)[0, :1] + y[:, unstriped(pos2)] * f64(gate)[1, :1] + y[:, unstriped(pos3)] * f64(gate)[2, :1]
    return (out_0,) + planes(out_0)

@@ -1,0 +1,227 @@
+from contextlib import ExitStack
+
+import concourse.mybir as mybir
+from concourse.masks import make_identity
+
+FLOPS = 805306368
+
+F32 = mybir.dt.float32
+BF16 = mybir.dt.bfloat16
+I32 = mybir.dt.int32
+U32 = mybir.dt.uint32
+U16 = mybir.dt.uint16
+U8 = mybir.dt.uint8
+FP8X4 = mybir.dt.float8_e4m3fn_x4
+FP4X4 = mybir.dt.float4_e2m1fn_x4
+ADD = mybir.AluOpType.add
+MULT = mybir.AluOpType.mult
+RELU = mybir.ActivationFunctionType.Relu
+COPY = mybir.ActivationFunctionType.Copy
+
+P = 128
+PACK = 4
+T, S, V, H, U, D = 2048, 512, 512, 512, 1024, 3
+HALF = 512
+
+
+def tile_picked_devox_none_po_kernel(
+    tc, x_words, x_scales, w1, w2_words, w2_scales, gate, emb, offs, cell, pos1, pos2, pos3, out_0, out_1, out_2
+):
+    nc = tc.nc
+    with ExitStack() as ctx:
+        lists = ctx.enter_context(tc.tile_pool(name="lists", bufs=1))
+        keep = ctx.enter_context(tc.tile_pool(name="keep", bufs=1))
+        ring = ctx.enter_context(tc.tile_pool(name="ring", bufs=2))
+        psum = ctx.enter_context(tc.psum_pool(name="psum", bufs=1))
+
+        def load_list(name, src):
+            tile = lists.tile([P, S // 16], U16, name=name)
+            nc.sync.dma_start(tile[:], src)
+            return tile
+
+        def load_scale_rows(queue, tile, rows):
+            for q in range(4):
+                queue.dma_start(tile[32 * q : 32 * q + 4, :].bitcast(I32), rows[0, 4 * q : 4 * q + 4, :].bitcast(I32))
+
+        x_scale_table = keep.tile([P, T], U8, name="x_scale_table", align_bytes=64)
+        nc.gpsimd.memset(x_scale_table[:].bitcast(I32), 0)
+        offs_t = load_list("offs", offs)
+        w1_raw = keep.tile([P, PACK, H], F32, name="w1_raw")
+        nc.sync.dma_start(w1_raw[:], w1.rearrange("(p j) c -> p j c", j=PACK))
+        load_scale_rows(nc.sync, x_scale_table, x_scales)
+        x_word_table = keep.tile([P, T], U32, name="x_word_table", align_bytes=64)
+        nc.sync.dma_start(x_word_table[:].bitcast(I32), x_words[0].rearrange("p n t -> p (n t)").bitcast(I32))
+        cell_t = load_list("cell", cell)
+
+        w2_raw = keep.tile([P, 2 * H], U8, name="w2_raw", align_bytes=64)
+        nc.sync.dma_start(w2_raw[:].bitcast(I32), w2_words[0].bitcast(I32))
+        w2_scale_raw = keep.tile([P, H], U8, name="w2_scale_raw", align_bytes=64)
+        nc.vector.memset(w2_scale_raw[:].bitcast(I32), 0)
+        load_scale_rows(nc.sync, w2_scale_raw, w2_scales)
+        emb_rows = emb.rearrange("(p t) c -> p t c", t=PACK)
+        emb_t = []
+        for t in range(PACK):
+            tile = keep.tile([P, U], F32, name=f"emb{t}")
+            nc.sync.dma_start(tile[:], emb_rows[:, t, :])
+            emb_t.append(tile)
+        pos_t = [load_list(f"pos{d + 1}", src) for d, src in enumerate((pos1, pos2, pos3))]
+        gate_t = []
+        for d in range(D):
+            tile = keep.tile([P, V], F32, name=f"gate{d}")
+            nc.sync.dma_start(tile[:], gate[d])
+            gate_t.append(tile)
+
+        windows = []
+        for t in range(2):
+            tile = keep.tile([P, U], F32, name=f"window{t}")
+            nc.vector.memset(tile[:], 0.0)
+            windows.append(tile)
+        identity = keep.tile([P, P], F32, name="identity")
+        make_identity(nc, identity[:])
+
+        x_scale = keep.tile([P, S], U8, name="x_scale", align_bytes=64)
+        nc.vector.tensor_copy(x_scale[:], x_scale_table[:].indirect(offs_t[:]))
+
+        w1_codes, w1_scale = [], []
+        w1_view = w1_raw[:].rearrange("p j (m t) -> p m j t", t=PACK)
+        for u in range(2):
+            grouped = keep.tile([P, 2, P, PACK], BF16, name=f"w1_grouped{u}", align_bytes=64)
+            dst = grouped[:].rearrange("p t m j -> p m j t")
+            src = w1_view[:, :, :, 2 * u : 2 * u + 2]
+            nc.scalar.activation(dst, src, COPY)
+            codes = keep.tile([P, 2 * P], U32, name=f"w1_codes{u}", align_bytes=64)
+            scale = keep.tile([P, 2 * P], U8, name=f"w1_scale{u}", align_bytes=64)
+            nc.vector.quantize_mx(
+                out=codes[:].bitcast(FP8X4), scales=scale[:], in_=grouped[:].rearrange("p t m j -> p (t m j)")
+            )
+            w1_codes.append(codes)
+            w1_scale.append(scale)
+
+        x_codes = []
+        for a in range(2):
+            tile = keep.tile([P, S // 2], U32, name=f"x_codes{a}", align_bytes=64)
+            nc.vector.tensor_copy(tile[:], x_word_table[:].indirect(offs_t[:, 16 * a : 16 * a + 16]))
+            x_codes.append(tile)
+
+        w2_codes = keep.tile([P, PACK, P, 2], U8, name="w2_codes", align_bytes=64)
+        nc.gpsimd.tensor_copy(
+            w2_codes[:].rearrange("p t m b -> p m t b"), w2_raw[:].rearrange("p (m t b) -> p m t b", t=PACK, b=2)
+        )
+        w2_scale = keep.tile([P, PACK, P], U8, name="w2_scale", align_bytes=64)
+        nc.gpsimd.tensor_copy(
+            w2_scale[:].rearrange("p t m -> p m t"), w2_scale_raw[:].rearrange("p (m t) -> p m t", t=PACK)
+        )
+
+        z_rows = keep.tile([P, PACK, U], BF16, name="z_rows", align_bytes=64)
+        z_grouped = [keep.tile([P, HALF, PACK], BF16, name=f"z_grouped{a}", align_bytes=64) for a in range(2)]
+
+        def place_pair(copy, grouped, rows, u):
+            copy(grouped[:, :, 2 * u : 2 * u + 2], rows[:, 2 * u : 2 * u + 2, :].rearrange("p e c -> p c e"))
+
+        for t in range(PACK):
+            cols = slice((t % 2) * P, (t % 2 + 1) * P)
+            h_parts = []
+            for a in range(2):
+                bank = psum.tile([P, S // 2], F32, name="h_bank", tag="h_bank", bufs=2)
+                nc.tensor.matmul_mx(
+                    out=bank[:],
+                    lhsT=w1_codes[t // 2][:, cols].bitcast(FP8X4),
+                    lhsT_scale=w1_scale[t // 2][:, cols],
+                    rhs=x_codes[a][:].bitcast(FP8X4),
+                    rhs_scale=x_scale[:, a * (S // 2) : (a + 1) * (S // 2)],
+                    start=True,
+                    stop=True,
+                )
+                h_parts.append(bank)
+            h = keep.tile([P, S], F32, name=f"h{t}")
+            for a in range(2):
+                nc.scalar.activation(h[:, a * (S // 2) : (a + 1) * (S // 2)], h_parts[a][:], RELU)
+            if t == 0:
+                for a in range(2):
+                    nc.vector.tensor_copy(
+                        windows[t % 2][:].indirect(cell_t[:, 16 * a : 16 * a + 16]), h[:, a * (S // 2) : (a + 1) * (S // 2)]
+                    )
+            else:
+                nc.vector.tensor_copy(windows[t % 2][:].indirect(cell_t[:]), h[:])
+            if t < PACK - 1:
+                nc.gpsimd.tensor_tensor(z_rows[:, t, :], windows[t % 2][:], emb_t[t][:], ADD)
+            else:
+                for a in range(2):
+                    cells = slice(a * HALF, (a + 1) * HALF)
+                    nc.vector.tensor_tensor(z_rows[:, t, cells], windows[t % 2][:, cells], emb_t[t][:, cells], ADD)
+            if t == 1:
+                for a in range(2):
+                    place_pair(nc.scalar.copy, z_grouped[a], z_rows[:, :, a * HALF : (a + 1) * HALF], 0)
+
+        z_codes, z_scale = [None, None], [None, None]
+        place_pair(nc.scalar.copy, z_grouped[0], z_rows[:, :, 0:HALF], 1)
+        place_pair(nc.vector.tensor_copy, z_grouped[1], z_rows[:, :, HALF:U], 1)
+        for a in (1, 0):
+            codes = keep.tile([P, HALF], U32, name=f"z_codes{a}", align_bytes=64)
+            scale = keep.tile([P, HALF], U8, name=f"z_scale{a}", align_bytes=64)
+            nc.vector.quantize_mx(
+                out=codes[:].bitcast(FP8X4), scales=scale[:], in_=z_grouped[a][:].rearrange("p c t -> p (c t)")
+            )
+            z_codes[a] = codes
+            z_scale[a] = scale
+
+        out_rows = out_0.rearrange("(p t) v -> p t v", t=PACK)
+        result = keep.tile([P, PACK, V], F32, name="result")
+        grouped = keep.tile([P, V, PACK], BF16, name="out_grouped", align_bytes=64)
+        for t in range(PACK):
+            y = keep.tile([P, U], F32, name=f"y{t}")
+            for a in (1, 0):
+                bank = psum.tile([P, HALF], F32, name="y_bank", tag="y_bank", bufs=4)
+                nc.tensor.matmul_mx(
+                    out=bank[:],
+                    lhsT=w2_codes[:, t, :, :].rearrange("p m b -> p (m b)").bitcast(FP4X4),
+                    lhsT_scale=w2_scale[:, t, :],
+                    rhs=z_codes[a][:].bitcast(FP8X4),
+                    rhs_scale=z_scale[a][:],
+                    start=True,
+                    stop=True,
+                )
+                if t == 0 and a == 0:
+                    nc.vector.tensor_copy(y[:, a * HALF : (a + 1) * HALF], bank[:])
+                else:
+                    nc.scalar.copy(y[:, a * HALF : (a + 1) * HALF], bank[:])
+            terms = []
+            for d in range(D):
+                term = ring.tile([P, V], F32, name=f"term{d}")
+                nc.vector.tensor_tensor(term[:], y[:].indirect(pos_t[d][:]), gate_t[d][:], MULT)
+                terms.append(term)
+                if t == PACK - 1 and d == 1:
+                    partial = keep.tile([P, V], F32, name="partial")
+                    nc.vector.tensor_tensor(partial[:], terms[0][:], terms[1][:], ADD)
+            if t == PACK - 1:
+                nc.vector.tensor_tensor(result[:, t, :], partial[:], terms[2][:], ADD)
+            else:
+                turned = psum.tile([P, V // P, P], F32, name="turned", tag="turned")
+                for b in range(V // P):
+                    for d in range(D):
+                        nc.tensor.matmul(
+                            turned[:, b, :],
+                            terms[d][:, b * P : (b + 1) * P],
+                            identity[:],
+                            start=(d == 0),
+                            stop=(d == D - 1),
+                            is_transpose=True,
+                        )
+                turned_sb = ring.tile([P, V // P, P], F32, name="turned_sb")
+                nc.scalar.copy(turned_sb[:], turned[:])
+                back = psum.tile([P, V // P, P], F32, name="back", tag="back")
+                for b in range(V // P):
+                    nc.tensor.transpose(back[:, b, :], turned_sb[:, b, :], identity[:])
+                nc.scalar.copy(result[:, t, :], back[:].rearrange("p b v -> p (b v)"))
+            nc.sync.dma_start(out_rows[:, t, :], result[:, t, :])
+            if t == 1:
+                place_pair(nc.scalar.copy, grouped, result, 0)
+
+        place_pair(nc.vector.tensor_copy, grouped, result, 1)
+        codes = keep.tile([P, V], U32, name="out_codes", align_bytes=64)
+        scale = keep.tile([P, V], U8, name="out_scale", align_bytes=64)
+        nc.vector.quantize_mx(out=codes[:].bitcast(FP8X4), scales=scale[:], in_=grouped[:].rearrange("p c t -> p (c t)"))
+        nc.sync.dma_start(out_1[0].rearrange("p n t -> p (n t)").bitcast(I32), codes[:].bitcast(I32))
+        for q in range(4):
+            queue = nc.scalar if q % 2 == 0 else nc.sync
+            queue.dma_start(out_2[0, 4 * q : 4 * q + 4, :].bitcast(I32), scale[32 * q : 32 * q + 4, :].bitcast(I32))

@@ -22,6 +22,8 @@ P = 128
 PACK = 4
 T, S, V, H, U, D = 2048, 512, 512, 512, 1024, 3
 HALF = 512
+BLOCKS = HALF // P
+QUARTER = 256
 
 
 def tile_picked_devox_none_po_kernel(
@@ -34,194 +36,243 @@ def tile_picked_devox_none_po_kernel(
         ring = ctx.enter_context(tc.tile_pool(name="ring", bufs=2))
         psum = ctx.enter_context(tc.psum_pool(name="psum", bufs=1))
 
+        def bank(k, columns=HALF):
+            return psum.tile([P, columns], F32, name=f"bank{k}", tag=f"bank{k}")
+
         def load_list(name, src):
             tile = lists.tile([P, S // 16], U16, name=name)
             nc.sync.dma_start(tile[:], src)
             return tile
 
-        def load_scale_rows(queue, tile, rows):
+        def load_scale_rows(tile, rows):
             for q in range(4):
-                queue.dma_start(tile[32 * q : 32 * q + 4, :].bitcast(I32), rows[0, 4 * q : 4 * q + 4, :].bitcast(I32))
+                nc.sync.dma_start(tile[32 * q : 32 * q + 4, :].bitcast(I32), rows[0, 4 * q : 4 * q + 4, :].bitcast(I32))
+
+        def mx_tiles(name, width):
+            codes = keep.tile([P, width], U32, name=f"{name}_codes", align_bytes=64)
+            scale = keep.tile([P, width], U8, name=f"{name}_scale", align_bytes=64)
+            return codes, scale
+
+        def quantize_into(codes, scale, grouped):
+            nc.vector.quantize_mx(out=codes.bitcast(FP8X4), scales=scale, in_=grouped)
+
+        def quantize(name, grouped):
+            codes, scale = mx_tiles(name, grouped.shape[1] // PACK)
+            quantize_into(codes[:], scale[:], grouped)
+            return codes, scale
+
+        def add_turned(target, source, first, last):
+            for b in range(BLOCKS):
+                cols = slice(b * P, (b + 1) * P)
+                nc.tensor.matmul(
+                    target[:, cols],
+                    source[:, cols],
+                    identity[:],
+                    start=(first and b == 0),
+                    stop=(last and b == BLOCKS - 1),
+                    is_transpose=True,
+                )
+
+        def place_pair(copy, grouped, pair, u):
+            copy(grouped[:, :, 2 * u : 2 * u + 2], pair.rearrange("p e c -> p c e"))
 
         x_scale_table = keep.tile([P, T], U8, name="x_scale_table", align_bytes=64)
         nc.gpsimd.memset(x_scale_table[:].bitcast(I32), 0)
+        w2_scale_raw = keep.tile([P, H], U8, name="w2_scale_raw", align_bytes=64)
+        nc.gpsimd.memset(w2_scale_raw[:].bitcast(I32), 0)
+        identity = keep.tile([P, P], F32, name="identity")
+        make_identity(nc, identity[:])
+
+        w1_rows = w1.rearrange("(p j) c -> p j c", j=PACK)
+        w1_raw = [keep.tile([P, PACK, H // 2], F32, name=f"w1_raw{h}", tag=f"w1_raw{h}") for h in range(2)]
         offs_t = load_list("offs", offs)
-        w1_raw = keep.tile([P, PACK, H], F32, name="w1_raw")
-        nc.sync.dma_start(w1_raw[:], w1.rearrange("(p j) c -> p j c", j=PACK))
-        load_scale_rows(nc.sync, x_scale_table, x_scales)
+        nc.sync.dma_start(w1_raw[0][:], w1_rows[:, :, 0 : H // 2])
+        load_scale_rows(x_scale_table, x_scales)
         x_word_table = keep.tile([P, T], U32, name="x_word_table", align_bytes=64)
         nc.sync.dma_start(x_word_table[:].bitcast(I32), x_words[0].rearrange("p n t -> p (n t)").bitcast(I32))
         cell_t = load_list("cell", cell)
+        nc.sync.dma_start(w1_raw[1][:], w1_rows[:, :, H // 2 : H])
 
+        emb_pairs = emb.rearrange("(h m t) c -> h t m c", h=2, t=PACK)
+        emb_rows = emb.rearrange("(p t) c -> p t c", t=PACK)
+        emb_t = [keep.tile([P, U], F32, name=f"emb{t}") for t in range(PACK)]
+        for h in range(2):
+            for e in range(2):
+                nc.sync.dma_start(emb_t[h][e:P:2, :], emb_pairs[h, e])
         w2_raw = keep.tile([P, 2 * H], U8, name="w2_raw", align_bytes=64)
         nc.sync.dma_start(w2_raw[:].bitcast(I32), w2_words[0].bitcast(I32))
-        w2_scale_raw = keep.tile([P, H], U8, name="w2_scale_raw", align_bytes=64)
-        nc.vector.memset(w2_scale_raw[:].bitcast(I32), 0)
-        load_scale_rows(nc.sync, w2_scale_raw, w2_scales)
-        emb_rows = emb.rearrange("(p t) c -> p t c", t=PACK)
-        emb_t = []
-        for t in range(PACK):
-            tile = keep.tile([P, U], F32, name=f"emb{t}")
-            nc.sync.dma_start(tile[:], emb_rows[:, t, :])
-            emb_t.append(tile)
+        load_scale_rows(w2_scale_raw, w2_scales)
         pos_t = [load_list(f"pos{d + 1}", src) for d, src in enumerate((pos1, pos2, pos3))]
         gate_t = []
         for d in range(D):
             tile = keep.tile([P, V], F32, name=f"gate{d}")
             nc.sync.dma_start(tile[:], gate[d])
             gate_t.append(tile)
+        for t in range(2, PACK):
+            nc.sync.dma_start(emb_t[t][:], emb_rows[:, t, :])
 
         windows = []
-        for t in range(2):
-            tile = keep.tile([P, U], F32, name=f"window{t}")
+        for w in range(3):
+            tile = keep.tile([P, U], F32, name=f"window{w}")
             nc.vector.memset(tile[:], 0.0)
             windows.append(tile)
-        identity = keep.tile([P, P], F32, name="identity")
-        make_identity(nc, identity[:])
-
-        x_scale = keep.tile([P, S], U8, name="x_scale", align_bytes=64)
-        nc.vector.tensor_copy(x_scale[:], x_scale_table[:].indirect(offs_t[:]))
-
-        w1_codes, w1_scale = [], []
-        w1_view = w1_raw[:].rearrange("p j (m t) -> p m j t", t=PACK)
-        for u in range(2):
-            grouped = keep.tile([P, 2, P, PACK], BF16, name=f"w1_grouped{u}", align_bytes=64)
-            dst = grouped[:].rearrange("p t m j -> p m j t")
-            src = w1_view[:, :, :, 2 * u : 2 * u + 2]
-            nc.scalar.activation(dst, src, COPY)
-            codes = keep.tile([P, 2 * P], U32, name=f"w1_codes{u}", align_bytes=64)
-            scale = keep.tile([P, 2 * P], U8, name=f"w1_scale{u}", align_bytes=64)
-            nc.vector.quantize_mx(
-                out=codes[:].bitcast(FP8X4), scales=scale[:], in_=grouped[:].rearrange("p t m j -> p (t m j)")
-            )
-            w1_codes.append(codes)
-            w1_scale.append(scale)
-
-        x_codes = []
-        for a in range(2):
-            tile = keep.tile([P, S // 2], U32, name=f"x_codes{a}", align_bytes=64)
-            nc.vector.tensor_copy(tile[:], x_word_table[:].indirect(offs_t[:, 16 * a : 16 * a + 16]))
-            x_codes.append(tile)
 
         w2_codes = keep.tile([P, PACK, P, 2], U8, name="w2_codes", align_bytes=64)
         nc.gpsimd.tensor_copy(
             w2_codes[:].rearrange("p t m b -> p m t b"), w2_raw[:].rearrange("p (m t b) -> p m t b", t=PACK, b=2)
         )
+
+        x_scale = keep.tile([P, S], U8, name="x_scale", align_bytes=64)
+        nc.vector.tensor_copy(x_scale[:], x_scale_table[:].indirect(offs_t[:]))
+
+        w1_low = [keep.tile([P, P // 2, 2, PACK], BF16, name=f"w1_low{h}", align_bytes=64) for h in range(2)]
+        w1_high = keep.tile([P, 2, P, PACK], BF16, name="w1_high", align_bytes=64)
+
+        def round_w1(h):
+            view = w1_raw[h][:].rearrange("p j (m t) -> p m j t", t=PACK)
+            nc.scalar.activation(w1_low[h][:].rearrange("p m e j -> p m j e"), view[:, :, :, 0:2], COPY)
+            rows = slice(h * (P // 2), (h + 1) * (P // 2))
+            nc.scalar.activation(w1_high[:, :, rows, :].rearrange("p t m j -> p m j t"), view[:, :, :, 2:4], COPY)
+
+        round_w1(0)
+        w1_mx = [quantize("w1_low0", w1_low[0][:].rearrange("p m e j -> p (m e j)"))]
+
+        x_codes = keep.tile([P, S], U32, name="x_codes", align_bytes=64)
+        for a in range(2):
+            nc.vector.tensor_copy(
+                x_codes[:, a * (S // 2) : (a + 1) * (S // 2)], x_word_table[:].indirect(offs_t[:, 16 * a : 16 * a + 16])
+            )
+
+        def first_layer(hidden, codes, scale, points, k):
+            acc = bank(k, points.stop - points.start)
+            nc.tensor.matmul_mx(
+                out=acc[:],
+                lhsT=codes.bitcast(FP8X4),
+                lhsT_scale=scale,
+                rhs=x_codes[:, points].bitcast(FP8X4),
+                rhs_scale=x_scale[:, points],
+                start=True,
+                stop=True,
+            )
+            nc.scalar.activation(hidden[:], acc[:], RELU)
+
+        first = keep.tile([P, S // 2], F32, name="h0_first")
+        first_layer(first, w1_mx[0][0][:], w1_mx[0][1][:], slice(0, S // 2), 0)
+        nc.vector.tensor_copy(windows[0][:].indirect(cell_t[:, 0:16]), first[:])
+        round_w1(1)
+        low_codes, low_scale = quantize("w1_low1", w1_low[1][:].rearrange("p m e j -> p (m e j)"))
+        high_codes, high_scale = quantize("w1_high", w1_high[:].rearrange("p t m j -> p (t m j)"))
+        second = keep.tile([P, S // 2], F32, name="h0_second", tag="w1_raw1")
+        first_layer(second, w1_mx[0][0][:], w1_mx[0][1][:], slice(S // 2, S), 1)
+        nc.vector.tensor_copy(windows[0][:].indirect(cell_t[:, 16:32]), second[:])
+        h_t = {t: keep.tile([P, S], F32, name=f"h{t}") for t in range(1, PACK)}
+        first_layer(h_t[1], low_codes[:], low_scale[:], slice(0, S), 0)
+        for t in range(2, PACK):
+            cols = slice((t - 2) * P, (t - 1) * P)
+            first_layer(h_t[t], high_codes[:, cols], high_scale[:, cols], slice(0, S), (t + 1) % 2)
+
         w2_scale = keep.tile([P, PACK, P], U8, name="w2_scale", align_bytes=64)
         nc.gpsimd.tensor_copy(
             w2_scale[:].rearrange("p t m -> p m t"), w2_scale_raw[:].rearrange("p (m t) -> p m t", t=PACK)
         )
 
-        z_rows = keep.tile([P, PACK, U], BF16, name="z_rows", align_bytes=64)
-        z_grouped = [keep.tile([P, HALF, PACK], BF16, name=f"z_grouped{a}", align_bytes=64) for a in range(2)]
-
-        def place_pair(copy, grouped, rows, u):
-            copy(grouped[:, :, 2 * u : 2 * u + 2], rows[:, 2 * u : 2 * u + 2, :].rearrange("p e c -> p c e"))
-
-        for t in range(PACK):
-            cols = slice((t % 2) * P, (t % 2 + 1) * P)
-            h_parts = []
+        z_grouped = [keep.tile([P, QUARTER, PACK], BF16, name=f"z_grouped{c}", align_bytes=64) for c in range(4)]
+        z_turned = [keep.tile([P, BLOCKS, 2, P], BF16, name=f"z_turned{a}", align_bytes=64) for a in range(2)]
+        for h in range(2):
+            if h == 1:
+                nc.vector.tensor_copy(windows[1][:].indirect(cell_t[:]), h_t[1][:])
             for a in range(2):
-                bank = psum.tile([P, S // 2], F32, name="h_bank", tag="h_bank", bufs=2)
-                nc.tensor.matmul_mx(
-                    out=bank[:],
-                    lhsT=w1_codes[t // 2][:, cols].bitcast(FP8X4),
-                    lhsT_scale=w1_scale[t // 2][:, cols],
-                    rhs=x_codes[a][:].bitcast(FP8X4),
-                    rhs_scale=x_scale[:, a * (S // 2) : (a + 1) * (S // 2)],
-                    start=True,
-                    stop=True,
-                )
-                h_parts.append(bank)
-            h = keep.tile([P, S], F32, name=f"h{t}")
-            for a in range(2):
-                nc.scalar.activation(h[:, a * (S // 2) : (a + 1) * (S // 2)], h_parts[a][:], RELU)
-            if t == 0:
-                for a in range(2):
-                    nc.vector.tensor_copy(
-                        windows[t % 2][:].indirect(cell_t[:, 16 * a : 16 * a + 16]), h[:, a * (S // 2) : (a + 1) * (S // 2)]
-                    )
-            else:
-                nc.vector.tensor_copy(windows[t % 2][:].indirect(cell_t[:]), h[:])
-            if t < PACK - 1:
-                nc.gpsimd.tensor_tensor(z_rows[:, t, :], windows[t % 2][:], emb_t[t][:], ADD)
-            else:
-                for a in range(2):
-                    cells = slice(a * HALF, (a + 1) * HALF)
-                    nc.vector.tensor_tensor(z_rows[:, t, cells], windows[t % 2][:, cells], emb_t[t][:, cells], ADD)
-            if t == 1:
-                for a in range(2):
-                    place_pair(nc.scalar.copy, z_grouped[a], z_rows[:, :, a * HALF : (a + 1) * HALF], 0)
+                cells = slice(a * HALF, (a + 1) * HALF)
+                turned = bank(2 + 2 * h + a)
+                add_turned(turned, emb_t[h][:, cells], True, False)
+                add_turned(turned, windows[h][:, cells], False, True)
+                nc.scalar.copy(z_turned[a][:, :, h, :], turned[:].rearrange("p (b q) -> p b q", q=P))
+        for a in range(2):
+            back = bank(6 + a)
+            words = z_turned[a][:].rearrange("p b h q -> p (b h q)").bitcast(F32)
+            for b in range(BLOCKS):
+                cols = slice(b * P, (b + 1) * P)
+                nc.tensor.transpose(back[:, cols], words[:, cols], identity[:])
+            for c in range(2):
+                target = z_grouped[2 * a + c][:].rearrange("p c t -> p (c t)").bitcast(F32)
+                nc.scalar.copy(target[:, 0 : 2 * QUARTER : 2], back[:, c * QUARTER : (c + 1) * QUARTER])
 
-        z_codes, z_scale = [None, None], [None, None]
-        place_pair(nc.scalar.copy, z_grouped[0], z_rows[:, :, 0:HALF], 1)
-        place_pair(nc.vector.tensor_copy, z_grouped[1], z_rows[:, :, HALF:U], 1)
-        for a in (1, 0):
-            codes = keep.tile([P, HALF], U32, name=f"z_codes{a}", align_bytes=64)
-            scale = keep.tile([P, HALF], U8, name=f"z_scale{a}", align_bytes=64)
-            nc.vector.quantize_mx(
-                out=codes[:].bitcast(FP8X4), scales=scale[:], in_=z_grouped[a][:].rearrange("p c t -> p (c t)")
-            )
-            z_codes[a] = codes
-            z_scale[a] = scale
+        z_rows = [keep.tile([P, 2, QUARTER], BF16, name=f"z_rows{c}", align_bytes=64) for c in range(4)]
+        nc.vector.tensor_copy(windows[2][:].indirect(cell_t[:]), h_t[2][:])
+        nc.vector.tensor_copy(windows[0][:].indirect(cell_t[:]), h_t[3][:])
+        for e in range(2):
+            for c in range(4):
+                cells = slice(c * QUARTER, (c + 1) * QUARTER)
+                (nc.gpsimd if e == 0 else nc.vector).tensor_tensor(z_rows[c][:, e, :], windows[2 - 2 * e][:, cells], emb_t[2 + e][:, cells], ADD)
+        for c in range(4):
+            place_pair(nc.scalar.copy if c < 2 else nc.vector.tensor_copy, z_grouped[c], z_rows[c][:], 1)
+        z_mx = {}
+        for c in (0, 2, 1, 3):
+            z_mx[c] = quantize(f"z{c}", z_grouped[c][:].rearrange("p c t -> p (c t)"))
 
         out_rows = out_0.rearrange("(p t) v -> p t v", t=PACK)
         result = keep.tile([P, PACK, V], F32, name="result")
-        grouped = keep.tile([P, V, PACK], BF16, name="out_grouped", align_bytes=64)
+        grouped = [keep.tile([P, V // 2, PACK], BF16, name=f"out_grouped{a}", align_bytes=64) for a in range(2)]
+        halves = [slice(a * (V // 2), (a + 1) * (V // 2)) for a in range(2)]
+        y_t = []
         for t in range(PACK):
             y = keep.tile([P, U], F32, name=f"y{t}")
-            for a in (1, 0):
-                bank = psum.tile([P, HALF], F32, name="y_bank", tag="y_bank", bufs=4)
-                nc.tensor.matmul_mx(
-                    out=bank[:],
-                    lhsT=w2_codes[:, t, :, :].rearrange("p m b -> p (m b)").bitcast(FP4X4),
-                    lhsT_scale=w2_scale[:, t, :],
-                    rhs=z_codes[a][:].bitcast(FP8X4),
-                    rhs_scale=z_scale[a][:],
-                    start=True,
-                    stop=True,
-                )
-                if t == 0 and a == 0:
-                    nc.vector.tensor_copy(y[:, a * HALF : (a + 1) * HALF], bank[:])
+            y_t.append(y)
+            pieces = [[0], [2], [1], [3]] if t == 0 else [[0, 1], [2, 3]]
+            for i, quarters in enumerate(pieces):
+                cells = slice(quarters[0] * QUARTER, (quarters[-1] + 1) * QUARTER)
+                acc = bank(2 + i if t == 0 else 2 + (2 * t + i) % 4, len(quarters) * QUARTER)
+                for k, c in enumerate(quarters):
+                    nc.tensor.matmul_mx(
+                        out=acc[:, k * QUARTER : (k + 1) * QUARTER],
+                        lhsT=w2_codes[:, t, :, :].rearrange("p m b -> p (m b)").bitcast(FP4X4),
+                        lhsT_scale=w2_scale[:, t, :],
+                        rhs=z_mx[c][0][:].bitcast(FP8X4),
+                        rhs_scale=z_mx[c][1][:],
+                        start=True,
+                        stop=True,
+                    )
+                if t == 0 and i == len(pieces) - 1:
+                    nc.vector.tensor_copy(y[:, cells], acc[:])
                 else:
-                    nc.scalar.copy(y[:, a * HALF : (a + 1) * HALF], bank[:])
+                    nc.scalar.copy(y[:, cells], acc[:])
+        for t in range(PACK):
+            y = y_t[t]
             terms = []
+            if t < PACK - 1:
+                turned = bank(t % 2)
             for d in range(D):
                 term = ring.tile([P, V], F32, name=f"term{d}")
                 nc.vector.tensor_tensor(term[:], y[:].indirect(pos_t[d][:]), gate_t[d][:], MULT)
                 terms.append(term)
-                if t == PACK - 1 and d == 1:
+                if t < PACK - 1:
+                    add_turned(turned, term[:], d == 0, d == D - 1)
+                elif d == 1:
                     partial = keep.tile([P, V], F32, name="partial")
                     nc.vector.tensor_tensor(partial[:], terms[0][:], terms[1][:], ADD)
             if t == PACK - 1:
-                nc.vector.tensor_tensor(result[:, t, :], partial[:], terms[2][:], ADD)
+                for half in halves:
+                    nc.vector.tensor_tensor(result[:, t, half], partial[:, half], terms[2][:, half], ADD)
             else:
-                turned = psum.tile([P, V // P, P], F32, name="turned", tag="turned")
-                for b in range(V // P):
-                    for d in range(D):
-                        nc.tensor.matmul(
-                            turned[:, b, :],
-                            terms[d][:, b * P : (b + 1) * P],
-                            identity[:],
-                            start=(d == 0),
-                            stop=(d == D - 1),
-                            is_transpose=True,
-                        )
-                turned_sb = ring.tile([P, V // P, P], F32, name="turned_sb")
+                turned_sb = ring.tile([P, V], F32, name="turned_sb")
                 nc.scalar.copy(turned_sb[:], turned[:])
-                back = psum.tile([P, V // P, P], F32, name="back", tag="back")
-                for b in range(V // P):
-                    nc.tensor.transpose(back[:, b, :], turned_sb[:, b, :], identity[:])
-                nc.scalar.copy(result[:, t, :], back[:].rearrange("p b v -> p (b v)"))
+                back = bank(6 + t % 2)
+                for b in range(BLOCKS):
+                    cols = slice(b * P, (b + 1) * P)
+                    nc.tensor.transpose(back[:, cols], turned_sb[:, cols], identity[:])
+                nc.scalar.copy(result[:, t, :], back[:])
             nc.sync.dma_start(out_rows[:, t, :], result[:, t, :])
             if t == 1:
-                place_pair(nc.scalar.copy, grouped, result, 0)
+                for a in range(2):
+                    place_pair(nc.scalar.copy, grouped[a], result[:, 0:2, halves[a]], 0)
 
-        place_pair(nc.vector.tensor_copy, grouped, result, 1)
-        codes = keep.tile([P, V], U32, name="out_codes", align_bytes=64)
-        scale = keep.tile([P, V], U8, name="out_scale", align_bytes=64)
-        nc.vector.quantize_mx(out=codes[:].bitcast(FP8X4), scales=scale[:], in_=grouped[:].rearrange("p c t -> p (c t)"))
-        nc.sync.dma_start(out_1[0].rearrange("p n t -> p (n t)").bitcast(I32), codes[:].bitcast(I32))
+        place_pair(nc.scalar.copy, grouped[0], result[:, 2:4, halves[0]], 1)
+        place_pair(nc.vector.tensor_copy, grouped[1], result[:, 2:4, halves[1]], 1)
+        codes, scale = mx_tiles("out", V)
+        out_words = out_1[0].rearrange("p n t -> p (n t)").bitcast(I32)
+        for a in (1, 0):
+            quantize_into(codes[:, halves[a]], scale[:, halves[a]], grouped[a][:].rearrange("p c t -> p (c t)"))
+            nc.sync.dma_start(out_words[:, halves[a]], codes[:, halves[a]].bitcast(I32))
         for q in range(4):
             queue = nc.scalar if q % 2 == 0 else nc.sync
             queue.dma_start(out_2[0, 4 * q : 4 * q + 4, :].bitcast(I32), scale[32 * q : 32 * q + 4, :].bitcast(I32))

@@ -102,14 +102,14 @@ def tile_picked_devox_none_po_kernel(
         w2_raw = keep.tile([P, 2 * H], U8, name="w2_raw", align_bytes=64)
         nc.sync.dma_start(w2_raw[:].bitcast(I32), w2_words[0].bitcast(I32))
         load_scale_rows(w2_scale_raw, w2_scales)
+        nc.sync.dma_start(emb_t[2][:], emb_rows[:, 2, :])
         pos_t = [load_list(f"pos{d + 1}", src) for d, src in enumerate((pos1, pos2, pos3))]
         gate_t = []
         for d in range(D):
             tile = keep.tile([P, V], F32, name=f"gate{d}")
             nc.sync.dma_start(tile[:], gate[d])
             gate_t.append(tile)
-        for t in range(2, PACK):
-            nc.sync.dma_start(emb_t[t][:], emb_rows[:, t, :])
+        nc.sync.dma_start(emb_t[3][:], emb_rows[:, 3, :])
 
         windows = []
         for w in range(3):
@@ -176,7 +176,8 @@ def tile_picked_devox_none_po_kernel(
             w2_scale[:].rearrange("p t m -> p m t"), w2_scale_raw[:].rearrange("p (m t) -> p m t", t=PACK)
         )
 
-        z_grouped = [keep.tile([P, QUARTER, PACK], BF16, name=f"z_grouped{c}", align_bytes=64) for c in range(4)]
+        z_halves = [keep.tile([P, HALF * PACK], BF16, name=f"z_half{a}", align_bytes=64) for a in range(2)]
+        z_grouped = [z_halves[c // 2][:, (c % 2) * QUARTER * PACK : (c % 2 + 1) * QUARTER * PACK] for c in range(4)]
         z_turned = [keep.tile([P, BLOCKS, 2, P], BF16, name=f"z_turned{a}", align_bytes=64) for a in range(2)]
         for h in range(2):
             if h == 1:
@@ -193,22 +194,39 @@ def tile_picked_devox_none_po_kernel(
             for b in range(BLOCKS):
                 cols = slice(b * P, (b + 1) * P)
                 nc.tensor.transpose(back[:, cols], words[:, cols], identity[:])
-            for c in range(2):
-                target = z_grouped[2 * a + c][:].rearrange("p c t -> p (c t)").bitcast(F32)
-                nc.scalar.copy(target[:, 0 : 2 * QUARTER : 2], back[:, c * QUARTER : (c + 1) * QUARTER])
+            nc.scalar.copy(
+                z_halves[a][:].bitcast(F32).rearrange("p (c u) -> p c u", u=2),
+                back[:].rearrange("p (c o) -> p c o", o=1).to_broadcast([P, HALF, 2]),
+            )
 
-        z_rows = [keep.tile([P, 2, QUARTER], BF16, name=f"z_rows{c}", align_bytes=64) for c in range(4)]
+        z_rows = keep.tile([P, 2 * U], BF16, name="z_rows", align_bytes=64)
+        z_pairs = z_rows[:].rearrange("p (c e n) -> p c e n", c=4, e=2)
         nc.vector.tensor_copy(windows[2][:].indirect(cell_t[:]), h_t[2][:])
         nc.vector.tensor_copy(windows[0][:].indirect(cell_t[:]), h_t[3][:])
-        for e in range(2):
-            for c in range(4):
-                cells = slice(c * QUARTER, (c + 1) * QUARTER)
-                (nc.gpsimd if e == 0 else nc.vector).tensor_tensor(z_rows[c][:, e, :], windows[2 - 2 * e][:, cells], emb_t[2 + e][:, cells], ADD)
+        nc.gpsimd.tensor_tensor(
+            z_pairs[:, :, 0, :],
+            windows[2][:].rearrange("p (c n) -> p c n", c=4),
+            emb_t[2][:].rearrange("p (c n) -> p c n", c=4),
+            ADD,
+        )
         for c in range(4):
-            place_pair(nc.scalar.copy if c < 2 else nc.vector.tensor_copy, z_grouped[c], z_rows[c][:], 1)
+            cells = slice(c * QUARTER, (c + 1) * QUARTER)
+            nc.vector.tensor_tensor(z_pairs[:, c, 1, :], windows[0][:, cells], emb_t[3][:, cells], ADD)
         z_mx = {}
-        for c in (0, 2, 1, 3):
-            z_mx[c] = quantize(f"z{c}", z_grouped[c][:].rearrange("p c t -> p (c t)"))
+
+        def place_z(copy, c):
+            place_pair(copy, z_grouped[c].rearrange("p (n t) -> p n t", t=PACK), z_pairs[:, c, :, :], 1)
+
+        def quantize_z(c):
+            z_mx[c] = quantize(f"z{c}", z_grouped[c])
+
+        place_z(nc.scalar.copy, 0)
+        place_z(nc.scalar.copy, 1)
+        place_z(nc.vector.tensor_copy, 2)
+        quantize_z(0)
+        place_z(nc.vector.tensor_copy, 3)
+        for c in (2, 1, 3):
+            quantize_z(c)
 
         out_rows = out_0.rearrange("(p t) v -> p t v", t=PACK)
         result = keep.tile([P, PACK, V], F32, name="result")
@@ -232,7 +250,7 @@ def tile_picked_devox_none_po_kernel(
                         start=True,
                         stop=True,
                     )
-                if t == 0 and i == len(pieces) - 1:
+                if t == 0 and i >= 2:
                     nc.vector.tensor_copy(y[:, cells], acc[:])
                 else:
                     nc.scalar.copy(y[:, cells], acc[:])

@@ -73,6 +73,18 @@ def tile_picked_devox_none_po_kernel(
                     is_transpose=True,
                 )
 
+        def turn_all(target, source, blocks, first, last):
+            for b in range(blocks):
+                cols = slice(b * P, (b + 1) * P)
+                nc.tensor.matmul(
+                    target[:, cols],
+                    source[:, cols],
+                    identity[:],
+                    start=(first and b == 0),
+                    stop=(last and b == blocks - 1),
+                    is_transpose=True,
+                )
+
         def place_pair(copy, grouped, pair, u):
             copy(grouped[:, :, 2 * u : 2 * u + 2], pair.rearrange("p e c -> p c e"))
 
@@ -95,21 +107,25 @@ def tile_picked_devox_none_po_kernel(
 
         emb_pairs = emb.rearrange("(h m t) c -> h t m c", h=2, t=PACK)
         emb_rows = emb.rearrange("(p t) c -> p t c", t=PACK)
-        emb_t = [keep.tile([P, U], F32, name=f"emb{t}") for t in range(PACK)]
+        emb_t = [keep.tile([P, U], F32, name=f"emb{t}") for t in range(PACK - 1)]
+        emb_head = keep.tile([P, 3 * QUARTER], F32, name="emb_head")
+        emb_tail = keep.tile([P, QUARTER], F32, name="emb_tail")
         for h in range(2):
             for e in range(2):
                 nc.sync.dma_start(emb_t[h][e:P:2, :], emb_pairs[h, e])
+            if h == 0:
+                nc.sync.dma_start(emb_head[:], emb_rows[:, 3, 0 : 3 * QUARTER])
         w2_raw = keep.tile([P, 2 * H], U8, name="w2_raw", align_bytes=64)
         nc.sync.dma_start(w2_raw[:].bitcast(I32), w2_words[0].bitcast(I32))
         load_scale_rows(w2_scale_raw, w2_scales)
         nc.sync.dma_start(emb_t[2][:], emb_rows[:, 2, :])
+        nc.sync.dma_start(emb_tail[:], emb_rows[:, 3, 3 * QUARTER : U])
         pos_t = [load_list(f"pos{d + 1}", src) for d, src in enumerate((pos1, pos2, pos3))]
         gate_t = []
         for d in range(D):
             tile = keep.tile([P, V], F32, name=f"gate{d}")
             nc.sync.dma_start(tile[:], gate[d])
             gate_t.append(tile)
-        nc.sync.dma_start(emb_t[3][:], emb_rows[:, 3, :])
 
         windows = []
         for w in range(3):
@@ -176,8 +192,19 @@ def tile_picked_devox_none_po_kernel(
             w2_scale[:].rearrange("p t m -> p m t"), w2_scale_raw[:].rearrange("p (m t) -> p m t", t=PACK)
         )
 
-        z_halves = [keep.tile([P, HALF * PACK], BF16, name=f"z_half{a}", align_bytes=64) for a in range(2)]
-        z_grouped = [z_halves[c // 2][:, (c % 2) * QUARTER * PACK : (c % 2 + 1) * QUARTER * PACK] for c in range(4)]
+        emb_turned = keep.tile([P, 3 * QUARTER], F32, name="emb_turned")
+        emb_banks = []
+        for a, cells in enumerate((slice(0, HALF), slice(HALF, HALF + QUARTER))):
+            width = cells.stop - cells.start
+            turned = bank(6 + a, width)
+            turn_all(turned, emb_head[:, cells], width // P, True, True)
+            nc.scalar.copy(emb_turned[:, cells], turned[:])
+            back = bank(a, width)
+            turn_all(back, emb_turned[:, cells], width // P, True, True)
+            emb_banks.append(back)
+
+        z_tiles = [keep.tile([P, QUARTER * PACK], BF16, name=f"z_quarter{c}", align_bytes=64) for c in range(4)]
+        z_grouped = [tile[:] for tile in z_tiles]
         z_turned = [keep.tile([P, BLOCKS, 2, P], BF16, name=f"z_turned{a}", align_bytes=64) for a in range(2)]
         for h in range(2):
             if h == 1:
@@ -194,53 +221,50 @@ def tile_picked_devox_none_po_kernel(
             for b in range(BLOCKS):
                 cols = slice(b * P, (b + 1) * P)
                 nc.tensor.transpose(back[:, cols], words[:, cols], identity[:])
-            nc.scalar.copy(
-                z_halves[a][:].bitcast(F32).rearrange("p (c u) -> p c u", u=2),
-                back[:].rearrange("p (c o) -> p c o", o=1).to_broadcast([P, HALF, 2]),
-            )
+            for c in (2 * a + 1, 2 * a):
+                part = back[:, (c % 2) * QUARTER : (c % 2 + 1) * QUARTER]
+                nc.scalar.copy(
+                    z_grouped[c].bitcast(F32).rearrange("p (c u) -> p c u", u=2),
+                    part.rearrange("p (c o) -> p c o", o=1).to_broadcast([P, QUARTER, 2]),
+                )
 
-        z_rows = keep.tile([P, 2 * U], BF16, name="z_rows", align_bytes=64)
-        z_pairs = z_rows[:].rearrange("p (c e n) -> p c e n", c=4, e=2)
+        z_rows = keep.tile([P, 3, 2, QUARTER], BF16, name="z_rows", align_bytes=64)
+        z_slots = [z_grouped[c].rearrange("p (n t) -> p n t", t=PACK) for c in range(4)]
+        quarter = [slice(c * QUARTER, (c + 1) * QUARTER) for c in range(4)]
         nc.vector.tensor_copy(windows[2][:].indirect(cell_t[:]), h_t[2][:])
         nc.vector.tensor_copy(windows[0][:].indirect(cell_t[:]), h_t[3][:])
         nc.gpsimd.tensor_tensor(
-            z_pairs[:, :, 0, :],
-            windows[2][:].rearrange("p (c n) -> p c n", c=4),
-            emb_t[2][:].rearrange("p (c n) -> p c n", c=4),
+            z_rows[:, :, 0, :],
+            windows[2][:, 0 : 3 * QUARTER].rearrange("p (c n) -> p c n", c=3),
+            emb_t[2][:, 0 : 3 * QUARTER].rearrange("p (c n) -> p c n", c=3),
             ADD,
         )
-        for c in range(4):
-            cells = slice(c * QUARTER, (c + 1) * QUARTER)
-            nc.vector.tensor_tensor(z_pairs[:, c, 1, :], windows[0][:, cells], emb_t[3][:, cells], ADD)
+        nc.gpsimd.tensor_tensor(z_slots[3][:, :, 2], windows[2][:, quarter[3]], emb_t[2][:, quarter[3]], ADD)
+        nc.gpsimd.tensor_tensor(z_slots[3][:, :, 3], windows[0][:, quarter[3]], emb_tail[:], ADD)
+        for c in range(3):
+            nc.vector.tensor_tensor(
+                z_rows[:, c, 1, :], windows[0][:, quarter[c]], emb_banks[c // 2][:, quarter[c % 2]], ADD
+            )
+        for c in range(3):
+            place_pair(nc.scalar.copy if c < 2 else nc.vector.tensor_copy, z_slots[c], z_rows[:, c, :, :], 1)
         z_mx = {}
-
-        def place_z(copy, c):
-            place_pair(copy, z_grouped[c].rearrange("p (n t) -> p n t", t=PACK), z_pairs[:, c, :, :], 1)
-
-        def quantize_z(c):
+        for c in (2, 0, 3, 1):
             z_mx[c] = quantize(f"z{c}", z_grouped[c])
-
-        place_z(nc.scalar.copy, 0)
-        place_z(nc.scalar.copy, 1)
-        place_z(nc.vector.tensor_copy, 2)
-        quantize_z(0)
-        place_z(nc.vector.tensor_copy, 3)
-        for c in (2, 1, 3):
-            quantize_z(c)
 
         out_rows = out_0.rearrange("(p t) v -> p t v", t=PACK)
         result = keep.tile([P, PACK, V], F32, name="result")
         grouped = [keep.tile([P, V // 2, PACK], BF16, name=f"out_grouped{a}", align_bytes=64) for a in range(2)]
         halves = [slice(a * (V // 2), (a + 1) * (V // 2)) for a in range(2)]
         y_t = []
+        y_banks = {1: (4, 5), 2: (2, 4), 3: (3, 2)}
         for t in range(PACK):
             y = keep.tile([P, U], F32, name=f"y{t}")
             y_t.append(y)
-            pieces = [[0], [2], [1], [3]] if t == 0 else [[0, 1], [2, 3]]
+            pieces = [[2], [0], [3], [1]] if t == 0 else [[0, 1], [2, 3]]
             for i, quarters in enumerate(pieces):
                 cells = slice(quarters[0] * QUARTER, (quarters[-1] + 1) * QUARTER)
-                acc = bank(2 + i if t == 0 else 2 + (2 * t + i) % 4, len(quarters) * QUARTER)
-                for k, c in enumerate(quarters):
+                acc = bank(2 + i if t == 0 else y_banks[t][i], len(quarters) * QUARTER)
+                for k, c in reversed(list(enumerate(quarters))):
                     nc.tensor.matmul_mx(
                         out=acc[:, k * QUARTER : (k + 1) * QUARTER],
                         lhsT=w2_codes[:, t, :, :].rearrange("p m b -> p (m b)").bitcast(FP4X4),
@@ -250,47 +274,54 @@ def tile_picked_devox_none_po_kernel(
                         start=True,
                         stop=True,
                     )
-                if t == 0 and i >= 2:
+                if t == 0 and i == 3:
                     nc.vector.tensor_copy(y[:, cells], acc[:])
                 else:
                     nc.scalar.copy(y[:, cells], acc[:])
-        for t in range(PACK):
-            y = y_t[t]
-            terms = []
-            if t < PACK - 1:
-                turned = bank(t % 2)
-            for d in range(D):
-                term = ring.tile([P, V], F32, name=f"term{d}")
-                nc.vector.tensor_tensor(term[:], y[:].indirect(pos_t[d][:]), gate_t[d][:], MULT)
-                terms.append(term)
-                if t < PACK - 1:
-                    add_turned(turned, term[:], d == 0, d == D - 1)
-                elif d == 1:
-                    partial = keep.tile([P, V], F32, name="partial")
-                    nc.vector.tensor_tensor(partial[:], terms[0][:], terms[1][:], ADD)
-            if t == PACK - 1:
-                for half in halves:
-                    nc.vector.tensor_tensor(result[:, t, half], partial[:, half], terms[2][:, half], ADD)
-            else:
-                turned_sb = ring.tile([P, V], F32, name="turned_sb")
-                nc.scalar.copy(turned_sb[:], turned[:])
-                back = bank(6 + t % 2)
-                for b in range(BLOCKS):
-                    cols = slice(b * P, (b + 1) * P)
-                    nc.tensor.transpose(back[:, cols], turned_sb[:, cols], identity[:])
-                nc.scalar.copy(result[:, t, :], back[:])
-            nc.sync.dma_start(out_rows[:, t, :], result[:, t, :])
-            if t == 1:
-                for a in range(2):
-                    place_pair(nc.scalar.copy, grouped[a], result[:, 0:2, halves[a]], 0)
+        def gated(t, d, cols):
+            term = ring.tile([P, cols.stop - cols.start], F32, name=f"term{d}")
+            offsets = pos_t[d][:, cols.start // 16 : cols.stop // 16]
+            nc.vector.tensor_tensor(term[:], y_t[t][:].indirect(offsets), gate_t[d][:, cols], MULT)
+            return term
 
+        def summed_by_transposes(t, cols):
+            width = cols.stop - cols.start
+            turned = bank(t % 2, width)
+            for d in range(D):
+                turn_all(turned, gated(t, d, cols)[:], width // P, d == 0, d == D - 1)
+            turned_sb = ring.tile([P, width], F32, name="turned_sb")
+            nc.scalar.copy(turned_sb[:], turned[:])
+            back = bank(6 + t % 2, width)
+            turn_all(back, turned_sb[:], width // P, True, True)
+            nc.scalar.copy(result[:, t, cols], back[:])
+
+        for t in range(2):
+            summed_by_transposes(t, slice(0, V))
+            nc.sync.dma_start(out_rows[:, t, :], result[:, t, :])
+        for a in range(2):
+            place_pair(nc.scalar.copy, grouped[a], result[:, 0:2, halves[a]], 0)
+        last = PACK - 1
+        summed_by_transposes(2, halves[0])
+        summed_by_transposes(last, halves[0])
+        nc.sync.dma_start(out_rows[:, 2:4, halves[0]], result[:, 2:4, halves[0]])
         place_pair(nc.scalar.copy, grouped[0], result[:, 2:4, halves[0]], 1)
-        place_pair(nc.vector.tensor_copy, grouped[1], result[:, 2:4, halves[1]], 1)
+        summed_by_transposes(2, halves[1])
+        terms = [gated(last, d, halves[1]) for d in range(2)]
+        partial = keep.tile([P, V // 2], F32, name="partial")
+        nc.vector.tensor_tensor(partial[:], terms[0][:], terms[1][:], ADD)
+        nc.vector.tensor_tensor(result[:, last, halves[1]], partial[:], gated(last, 2, halves[1])[:], ADD)
+        nc.sync.dma_start(out_rows[:, 2:4, halves[1]], result[:, 2:4, halves[1]])
+
         codes, scale = mx_tiles("out", V)
         out_words = out_1[0].rearrange("p n t -> p (n t)").bitcast(I32)
-        for a in (1, 0):
+
+        def hand_on(a):
             quantize_into(codes[:, halves[a]], scale[:, halves[a]], grouped[a][:].rearrange("p c t -> p (c t)"))
             nc.sync.dma_start(out_words[:, halves[a]], codes[:, halves[a]].bitcast(I32))
+
+        place_pair(nc.vector.tensor_copy, grouped[1], result[:, 2:4, halves[1]], 1)
+        hand_on(0)
+        hand_on(1)
         for q in range(4):
             queue = nc.scalar if q % 2 == 0 else nc.sync
             queue.dma_start(out_2[0, 4 * q : 4 * q + 4, :].bitcast(I32), scale[32 * q : 32 * q + 4, :].bitcast(I32))

@@ -133,16 +133,12 @@ def tile_picked_devox_none_po_kernel(
             nc.vector.memset(tile[:], 0.0)
             windows.append(tile)
 
-        w2_codes = keep.tile([P, PACK, P, 2], U8, name="w2_codes", align_bytes=64)
-        nc.gpsimd.tensor_copy(
-            w2_codes[:].rearrange("p t m b -> p m t b"), w2_raw[:].rearrange("p (m t b) -> p m t b", t=PACK, b=2)
-        )
 
         x_scale = keep.tile([P, S], U8, name="x_scale", align_bytes=64)
         nc.vector.tensor_copy(x_scale[:], x_scale_table[:].indirect(offs_t[:]))
 
-        w1_low = [keep.tile([P, P // 2, 2, PACK], BF16, name=f"w1_low{h}", align_bytes=64) for h in range(2)]
-        w1_high = keep.tile([P, 2, P, PACK], BF16, name="w1_high", align_bytes=64)
+        w1_low = [keep.tile([P, P // 2, 2, PACK], BF16, name=f"w1_low{h}", tag=f"w1_low{h}", align_bytes=64) for h in range(2)]
+        w1_high = keep.tile([P, 2, P, PACK], BF16, name="w1_high", tag="w1_high", align_bytes=64)
 
         def round_w1(h):
             view = w1_raw[h][:].rearrange("p j (m t) -> p m j t", t=PACK)
@@ -187,7 +183,11 @@ def tile_picked_devox_none_po_kernel(
             cols = slice((t - 2) * P, (t - 1) * P)
             first_layer(h_t[t], high_codes[:, cols], high_scale[:, cols], slice(0, S), (t + 1) % 2)
 
-        w2_scale = keep.tile([P, PACK, P], U8, name="w2_scale", align_bytes=64)
+        w2_codes = keep.tile([P, PACK, P, 2], U8, name="w2_codes", tag="w1_high", align_bytes=64)
+        nc.gpsimd.tensor_copy(
+            w2_codes[:].rearrange("p t m b -> p m t b"), w2_raw[:].rearrange("p (m t b) -> p m t b", t=PACK, b=2)
+        )
+        w2_scale = keep.tile([P, PACK, P], U8, name="w2_scale", tag="w1_low1", align_bytes=64)
         nc.gpsimd.tensor_copy(
             w2_scale[:].rearrange("p t m -> p m t"), w2_scale_raw[:].rearrange("p (m t) -> p m t", t=PACK)
         )
@@ -241,43 +241,55 @@ def tile_picked_devox_none_po_kernel(
         )
         nc.gpsimd.tensor_tensor(z_slots[3][:, :, 2], windows[2][:, quarter[3]], emb_t[2][:, quarter[3]], ADD)
         nc.gpsimd.tensor_tensor(z_slots[3][:, :, 3], windows[0][:, quarter[3]], emb_tail[:], ADD)
-        for c in range(3):
+        for c in (0, 2, 1):
             nc.vector.tensor_tensor(
                 z_rows[:, c, 1, :], windows[0][:, quarter[c]], emb_banks[c // 2][:, quarter[c % 2]], ADD
             )
         for c in range(3):
             place_pair(nc.scalar.copy if c < 2 else nc.vector.tensor_copy, z_slots[c], z_rows[:, c, :, :], 1)
         z_mx = {}
-        for c in (2, 0, 3, 1):
+        for c in (2, 0, 3):
             z_mx[c] = quantize(f"z{c}", z_grouped[c])
+        z_mx[1] = mx_tiles("z1", QUARTER)
+        for a in range(2):
+            cols = slice(a * P, (a + 1) * P)
+            quantize_into(z_mx[1][0][:, cols], z_mx[1][1][:, cols], z_grouped[1][:, a * HALF : (a + 1) * HALF])
 
         out_rows = out_0.rearrange("(p t) v -> p t v", t=PACK)
         result = keep.tile([P, PACK, V], F32, name="result")
         grouped = [keep.tile([P, V // 2, PACK], BF16, name=f"out_grouped{a}", align_bytes=64) for a in range(2)]
         halves = [slice(a * (V // 2), (a + 1) * (V // 2)) for a in range(2)]
+
+        def second_layer(acc, t, c, cols):
+            nc.tensor.matmul_mx(
+                out=acc,
+                lhsT=w2_codes[:, t, :, :].rearrange("p m b -> p (m b)").bitcast(FP4X4),
+                lhsT_scale=w2_scale[:, t, :],
+                rhs=z_mx[c][0][:, cols].bitcast(FP8X4),
+                rhs_scale=z_mx[c][1][:, cols],
+                start=True,
+                stop=True,
+            )
+
         y_t = []
-        y_banks = {1: (4, 5), 2: (2, 4), 3: (3, 2)}
+        y_banks = {1: (4, 6), 2: (2, 4), 3: (3, 2)}
         for t in range(PACK):
             y = keep.tile([P, U], F32, name=f"y{t}")
             y_t.append(y)
-            pieces = [[2], [0], [3], [1]] if t == 0 else [[0, 1], [2, 3]]
-            for i, quarters in enumerate(pieces):
-                cells = slice(quarters[0] * QUARTER, (quarters[-1] + 1) * QUARTER)
-                acc = bank(2 + i if t == 0 else y_banks[t][i], len(quarters) * QUARTER)
-                for k, c in reversed(list(enumerate(quarters))):
-                    nc.tensor.matmul_mx(
-                        out=acc[:, k * QUARTER : (k + 1) * QUARTER],
-                        lhsT=w2_codes[:, t, :, :].rearrange("p m b -> p (m b)").bitcast(FP4X4),
-                        lhsT_scale=w2_scale[:, t, :],
-                        rhs=z_mx[c][0][:].bitcast(FP8X4),
-                        rhs_scale=z_mx[c][1][:],
-                        start=True,
-                        stop=True,
-                    )
-                if t == 0 and i == 3:
-                    nc.vector.tensor_copy(y[:, cells], acc[:])
-                else:
-                    nc.scalar.copy(y[:, cells], acc[:])
+            if t == 0:
+                pieces = [(2, 0, QUARTER), (0, 0, QUARTER), (3, 0, QUARTER), (1, 0, P), (1, P, QUARTER)]
+                for i, (c, lo, hi) in enumerate(pieces):
+                    acc = bank(2 + i, hi - lo)
+                    second_layer(acc[:], t, c, slice(lo, hi))
+                    copy = nc.vector.tensor_copy if i == len(pieces) - 1 else nc.scalar.copy
+                    copy(y[:, c * QUARTER + lo : c * QUARTER + hi], acc[:])
+            else:
+                for a in range(2):
+                    acc = bank(y_banks[t][a])
+                    for k in (1, 0):
+                        second_layer(acc[:, k * QUARTER : (k + 1) * QUARTER], t, 2 * a + k, slice(0, QUARTER))
+                    nc.scalar.copy(y[:, a * HALF : (a + 1) * HALF], acc[:])
+
         def gated(t, d, cols):
             term = ring.tile([P, cols.stop - cols.start], F32, name=f"term{d}")
             offsets = pos_t[d][:, cols.start // 16 : cols.stop // 16]
@@ -295,22 +307,21 @@ def tile_picked_devox_none_po_kernel(
             turn_all(back, turned_sb[:], width // P, True, True)
             nc.scalar.copy(result[:, t, cols], back[:])
 
-        for t in range(2):
+        last = PACK - 1
+        for t in range(last):
             summed_by_transposes(t, slice(0, V))
             nc.sync.dma_start(out_rows[:, t, :], result[:, t, :])
-        for a in range(2):
-            place_pair(nc.scalar.copy, grouped[a], result[:, 0:2, halves[a]], 0)
-        last = PACK - 1
-        summed_by_transposes(2, halves[0])
-        summed_by_transposes(last, halves[0])
-        nc.sync.dma_start(out_rows[:, 2:4, halves[0]], result[:, 2:4, halves[0]])
-        place_pair(nc.scalar.copy, grouped[0], result[:, 2:4, halves[0]], 1)
-        summed_by_transposes(2, halves[1])
-        terms = [gated(last, d, halves[1]) for d in range(2)]
-        partial = keep.tile([P, V // 2], F32, name="partial")
+            if t == 1:
+                for a in range(2):
+                    place_pair(nc.scalar.copy, grouped[a], result[:, 0:2, halves[a]], 0)
+        terms = [gated(last, d, slice(0, V)) for d in range(2)]
+        partial = keep.tile([P, V], F32, name="partial")
         nc.vector.tensor_tensor(partial[:], terms[0][:], terms[1][:], ADD)
-        nc.vector.tensor_tensor(result[:, last, halves[1]], partial[:], gated(last, 2, halves[1])[:], ADD)
-        nc.sync.dma_start(out_rows[:, 2:4, halves[1]], result[:, 2:4, halves[1]])
+        term = gated(last, 2, slice(0, V))
+        for half in halves:
+            nc.vector.tensor_tensor(result[:, last, half], partial[:, half], term[:, half], ADD)
+        nc.sync.dma_start(out_rows[:, last, :], result[:, last, :])
+        place_pair(nc.scalar.copy, grouped[0], result[:, 2:4, halves[0]], 1)
 
         codes, scale = mx_tiles("out", V)
         out_words = out_1[0].rearrange("p n t -> p (n t)").bitcast(I32)
@@ -320,8 +331,8 @@ def tile_picked_devox_none_po_kernel(
             nc.sync.dma_start(out_words[:, halves[a]], codes[:, halves[a]].bitcast(I32))
 
         place_pair(nc.vector.tensor_copy, grouped[1], result[:, 2:4, halves[1]], 1)
-        hand_on(0)
         hand_on(1)
+        hand_on(0)
         for q in range(4):
             queue = nc.scalar if q % 2 == 0 else nc.sync
             queue.dma_start(out_2[0, 4 * q : 4 * q + 4, :].bitcast(I32), scale[32 * q : 32 * q + 4, :].bitcast(I32))

@@ -301,7 +301,7 @@ def tile_picked_devox_none_po_kernel(
             turned = bank(t % 2, width)
             for d in range(D):
                 turn_all(turned, gated(t, d, cols)[:], width // P, d == 0, d == D - 1)
-            turned_sb = ring.tile([P, width], F32, name="turned_sb")
+            turned_sb = keep.tile([P, width], F32, name=f"turned_sb{t}", tag=f"sum{t}")
             nc.scalar.copy(turned_sb[:], turned[:])
             back = bank(6 + t % 2, width)
             turn_all(back, turned_sb[:], width // P, True, True)
@@ -314,13 +314,13 @@ def tile_picked_devox_none_po_kernel(
             if t == 1:
                 for a in range(2):
                     place_pair(nc.scalar.copy, grouped[a], result[:, 0:2, halves[a]], 0)
-        terms = [gated(last, d, slice(0, V)) for d in range(2)]
-        partial = keep.tile([P, V], F32, name="partial")
-        nc.vector.tensor_tensor(partial[:], terms[0][:], terms[1][:], ADD)
-        term = gated(last, 2, slice(0, V))
+        terms = [gated(last, d, slice(0, V)) for d in range(D)]
+        partial = keep.tile([P, V], F32, name="partial", tag=f"sum{last - 1}")
         for half in halves:
-            nc.vector.tensor_tensor(result[:, last, half], partial[:, half], term[:, half], ADD)
-        nc.sync.dma_start(out_rows[:, last, :], result[:, last, :])
+            nc.vector.tensor_tensor(partial[:, half], terms[0][:, half], terms[1][:, half], ADD)
+        for half in halves:
+            nc.vector.tensor_tensor(result[:, last, half], partial[:, half], terms[2][:, half], ADD)
+            nc.sync.dma_start(out_rows[:, last, half], result[:, last, half])
         place_pair(nc.scalar.copy, grouped[0], result[:, 2:4, halves[0]], 1)
 
         codes, scale = mx_tiles("out", V)

@@ -281,7 +281,7 @@ def tile_picked_devox_none_po_kernel(
                 for i, (c, lo, hi) in enumerate(pieces):
                     acc = bank(2 + i, hi - lo)
                     second_layer(acc[:], t, c, slice(lo, hi))
-                    copy = nc.vector.tensor_copy if i == len(pieces) - 1 else nc.scalar.copy
+                    copy = nc.vector.tensor_copy if i == len(pieces) - 2 else nc.scalar.copy
                     copy(y[:, c * QUARTER + lo : c * QUARTER + hi], acc[:])
             else:
                 for a in range(2):

@@ -247,26 +247,25 @@ def tile_picked_devox_none_po_kernel(
             )
         for c in range(3):
             place_pair(nc.scalar.copy if c < 2 else nc.vector.tensor_copy, z_slots[c], z_rows[:, c, :, :], 1)
-        z_mx = {}
+        z_codes, z_scale = mx_tiles("z", U)
         for c in (2, 0, 3):
-            z_mx[c] = quantize(f"z{c}", z_grouped[c])
-        z_mx[1] = mx_tiles("z1", QUARTER)
+            quantize_into(z_codes[:, quarter[c]], z_scale[:, quarter[c]], z_grouped[c])
         for a in range(2):
-            cols = slice(a * P, (a + 1) * P)
-            quantize_into(z_mx[1][0][:, cols], z_mx[1][1][:, cols], z_grouped[1][:, a * HALF : (a + 1) * HALF])
+            cells = slice(QUARTER + a * P, QUARTER + (a + 1) * P)
+            quantize_into(z_codes[:, cells], z_scale[:, cells], z_grouped[1][:, a * HALF : (a + 1) * HALF])
 
         out_rows = out_0.rearrange("(p t) v -> p t v", t=PACK)
         result = keep.tile([P, PACK, V], F32, name="result")
-        grouped = [keep.tile([P, V // 2, PACK], BF16, name=f"out_grouped{a}", align_bytes=64) for a in range(2)]
+        grouped = [keep.tile([P, V // 2, PACK], BF16, name="out_grouped0", align_bytes=64)]
         halves = [slice(a * (V // 2), (a + 1) * (V // 2)) for a in range(2)]
 
-        def second_layer(acc, t, c, cols):
+        def second_layer(acc, t, cells):
             nc.tensor.matmul_mx(
                 out=acc,
                 lhsT=w2_codes[:, t, :, :].rearrange("p m b -> p (m b)").bitcast(FP4X4),
                 lhsT_scale=w2_scale[:, t, :],
-                rhs=z_mx[c][0][:, cols].bitcast(FP8X4),
-                rhs_scale=z_mx[c][1][:, cols],
+                rhs=z_codes[:, cells].bitcast(FP8X4),
+                rhs_scale=z_scale[:, cells],
                 start=True,
                 stop=True,
             )
@@ -280,29 +279,34 @@ def tile_picked_devox_none_po_kernel(
                 pieces = [(2, 0, QUARTER), (0, 0, QUARTER), (3, 0, QUARTER), (1, 0, P), (1, P, QUARTER)]
                 for i, (c, lo, hi) in enumerate(pieces):
                     acc = bank(2 + i, hi - lo)
-                    second_layer(acc[:], t, c, slice(lo, hi))
+                    second_layer(acc[:], t, slice(c * QUARTER + lo, c * QUARTER + hi))
                     copy = nc.vector.tensor_copy if i == len(pieces) - 2 else nc.scalar.copy
                     copy(y[:, c * QUARTER + lo : c * QUARTER + hi], acc[:])
             else:
                 for a in range(2):
                     acc = bank(y_banks[t][a])
-                    for k in (1, 0):
-                        second_layer(acc[:, k * QUARTER : (k + 1) * QUARTER], t, 2 * a + k, slice(0, QUARTER))
+                    second_layer(acc[:], t, slice(a * HALF, (a + 1) * HALF))
                     nc.scalar.copy(y[:, a * HALF : (a + 1) * HALF], acc[:])
 
         def gated(t, d, cols):
-            term = ring.tile([P, cols.stop - cols.start], F32, name=f"term{d}")
+            if (t, d) == (2, D - 1):
+                term = keep.tile([P, V], F32, name="held_term", tag="held_term", align_bytes=64)
+            else:
+                term = ring.tile([P, cols.stop - cols.start], F32, name=f"term{d}")
             offsets = pos_t[d][:, cols.start // 16 : cols.stop // 16]
             nc.vector.tensor_tensor(term[:], y_t[t][:].indirect(offsets), gate_t[d][:, cols], MULT)
             return term
 
         def summed_by_transposes(t, cols):
             width = cols.stop - cols.start
-            turned = bank(t % 2, width)
+            turned = bank(min(t, 1), width)
             for d in range(D):
                 turn_all(turned, gated(t, d, cols)[:], width // P, d == 0, d == D - 1)
             turned_sb = keep.tile([P, width], F32, name=f"turned_sb{t}", tag=f"sum{t}")
             nc.scalar.copy(turned_sb[:], turned[:])
+            if t == 2:
+                grouped.append(keep.tile([P, V // 2, PACK], BF16, name="out_grouped1", tag="held_term", align_bytes=64))
+                place_pair(nc.scalar.copy, grouped[1], result[:, 0:2, halves[1]], 0)
             back = bank(6 + t % 2, width)
             turn_all(back, turned_sb[:], width // P, True, True)
             nc.scalar.copy(result[:, t, cols], back[:])
@@ -312,8 +316,7 @@ def tile_picked_devox_none_po_kernel(
             summed_by_transposes(t, slice(0, V))
             nc.sync.dma_start(out_rows[:, t, :], result[:, t, :])
             if t == 1:
-                for a in range(2):
-                    place_pair(nc.scalar.copy, grouped[a], result[:, 0:2, halves[a]], 0)
+                place_pair(nc.scalar.copy, grouped[0], result[:, 0:2, halves[0]], 0)
         terms = [gated(last, d, slice(0, V)) for d in range(D)]
         partial = keep.tile([P, V], F32, name="partial", tag=f"sum{last - 1}")
         for half in halves:

@@ -102,8 +102,8 @@ def tile_picked_devox_none_po_kernel(
         load_scale_rows(x_scale_table, x_scales)
         x_word_table = keep.tile([P, T], U32, name="x_word_table", align_bytes=64)
         nc.sync.dma_start(x_word_table[:].bitcast(I32), x_words[0].rearrange("p n t -> p (n t)").bitcast(I32))
-        cell_t = load_list("cell", cell)
         nc.sync.dma_start(w1_raw[1][:], w1_rows[:, :, H // 2 : H])
+        cell_t = load_list("cell", cell)
 
         emb_pairs = emb.rearrange("(h m t) c -> h t m c", h=2, t=PACK)
         emb_rows = emb.rearrange("(p t) c -> p t c", t=PACK)
@@ -140,13 +140,17 @@ def tile_picked_devox_none_po_kernel(
         w1_low = [keep.tile([P, P // 2, 2, PACK], BF16, name=f"w1_low{h}", tag=f"w1_low{h}", align_bytes=64) for h in range(2)]
         w1_high = keep.tile([P, 2, P, PACK], BF16, name="w1_high", tag="w1_high", align_bytes=64)
 
-        def round_w1(h):
+        def round_low(copy, h):
             view = w1_raw[h][:].rearrange("p j (m t) -> p m j t", t=PACK)
-            nc.scalar.activation(w1_low[h][:].rearrange("p m e j -> p m j e"), view[:, :, :, 0:2], COPY)
+            copy(w1_low[h][:].rearrange("p m e j -> p m j e"), view[:, :, :, 0:2])
+
+        def round_high(h):
+            view = w1_raw[h][:].rearrange("p j (m t) -> p m j t", t=PACK)
             rows = slice(h * (P // 2), (h + 1) * (P // 2))
             nc.scalar.activation(w1_high[:, :, rows, :].rearrange("p t m j -> p m j t"), view[:, :, :, 2:4], COPY)
 
-        round_w1(0)
+        round_low(nc.scalar.copy, 0)
+        round_high(0)
         w1_mx = [quantize("w1_low0", w1_low[0][:].rearrange("p m e j -> p (m e j)"))]
 
         x_codes = keep.tile([P, S], U32, name="x_codes", align_bytes=64)
@@ -155,33 +159,36 @@ def tile_picked_devox_none_po_kernel(
                 x_codes[:, a * (S // 2) : (a + 1) * (S // 2)], x_word_table[:].indirect(offs_t[:, 16 * a : 16 * a + 16])
             )
 
-        def first_layer(hidden, codes, scale, points, k):
-            acc = bank(k, points.stop - points.start)
-            nc.tensor.matmul_mx(
-                out=acc[:],
-                lhsT=codes.bitcast(FP8X4),
-                lhsT_scale=scale,
-                rhs=x_codes[:, points].bitcast(FP8X4),
-                rhs_scale=x_scale[:, points],
-                start=True,
-                stop=True,
-            )
+        def first_layer(hidden, codes, scale, pieces, k):
+            start = pieces[0].start
+            acc = bank(k, pieces[-1].stop - start)
+            for points in pieces:
+                nc.tensor.matmul_mx(
+                    out=acc[:, points.start - start : points.stop - start],
+                    lhsT=codes.bitcast(FP8X4),
+                    lhsT_scale=scale,
+                    rhs=x_codes[:, points].bitcast(FP8X4),
+                    rhs_scale=x_scale[:, points],
+                    start=True,
+                    stop=True,
+                )
             nc.scalar.activation(hidden[:], acc[:], RELU)
 
-        first = keep.tile([P, S // 2], F32, name="h0_first")
-        first_layer(first, w1_mx[0][0][:], w1_mx[0][1][:], slice(0, S // 2), 0)
-        nc.vector.tensor_copy(windows[0][:].indirect(cell_t[:, 0:16]), first[:])
-        round_w1(1)
+        round_low(nc.vector.tensor_copy, 1)
+        first = keep.tile([P, P], F32, name="h0_first")
+        first_layer(first, w1_mx[0][0][:], w1_mx[0][1][:], [slice(0, P)], 0)
+        nc.vector.tensor_copy(windows[0][:].indirect(cell_t[:, 0:8]), first[:])
         low_codes, low_scale = quantize("w1_low1", w1_low[1][:].rearrange("p m e j -> p (m e j)"))
+        round_high(1)
         high_codes, high_scale = quantize("w1_high", w1_high[:].rearrange("p t m j -> p (t m j)"))
-        second = keep.tile([P, S // 2], F32, name="h0_second", tag="w1_raw1")
-        first_layer(second, w1_mx[0][0][:], w1_mx[0][1][:], slice(S // 2, S), 1)
-        nc.vector.tensor_copy(windows[0][:].indirect(cell_t[:, 16:32]), second[:])
+        second = keep.tile([P, S - P], F32, name="h0_second", tag="w1_raw1")
+        first_layer(second, w1_mx[0][0][:], w1_mx[0][1][:], [slice(P, 2 * P), slice(2 * P, S)], 1)
+        nc.vector.tensor_copy(windows[0][:].indirect(cell_t[:, 8:32]), second[:])
         h_t = {t: keep.tile([P, S], F32, name=f"h{t}") for t in range(1, PACK)}
-        first_layer(h_t[1], low_codes[:], low_scale[:], slice(0, S), 0)
+        first_layer(h_t[1], low_codes[:], low_scale[:], [slice(0, S)], 0)
         for t in range(2, PACK):
             cols = slice((t - 2) * P, (t - 1) * P)
-            first_layer(h_t[t], high_codes[:, cols], high_scale[:, cols], slice(0, S), (t + 1) % 2)
+            first_layer(h_t[t], high_codes[:, cols], high_scale[:, cols], [slice(0, S)], (t + 1) % 2)
 
         w2_codes = keep.tile([P, PACK, P, 2], U8, name="w2_codes", tag="w1_high", align_bytes=64)
         nc.gpsimd.tensor_copy(
@@ -302,13 +309,14 @@ def tile_picked_devox_none_po_kernel(
             turned = bank(min(t, 1), width)
             for d in range(D):
                 turn_all(turned, gated(t, d, cols)[:], width // P, d == 0, d == D - 1)
-            turned_sb = keep.tile([P, width], F32, name=f"turned_sb{t}", tag=f"sum{t}")
-            nc.scalar.copy(turned_sb[:], turned[:])
+            back = bank(6 + t % 2, width)
+            for a, part in enumerate(halves if t == 2 else [cols]):
+                turned_sb = keep.tile([P, part.stop - part.start], F32, name=f"turned_sb{t}_{a}", tag=f"sum{t}_{a}")
+                nc.scalar.copy(turned_sb[:], turned[:, part])
+                turn_all(back[:, part], turned_sb[:], (part.stop - part.start) // P, True, True)
             if t == 2:
                 grouped.append(keep.tile([P, V // 2, PACK], BF16, name="out_grouped1", tag="held_term", align_bytes=64))
                 place_pair(nc.scalar.copy, grouped[1], result[:, 0:2, halves[1]], 0)
-            back = bank(6 + t % 2, width)
-            turn_all(back, turned_sb[:], width // P, True, True)
             nc.scalar.copy(result[:, t, cols], back[:])
 
         last = PACK - 1
@@ -317,25 +325,49 @@ def tile_picked_devox_none_po_kernel(
             nc.sync.dma_start(out_rows[:, t, :], result[:, t, :])
             if t == 1:
                 place_pair(nc.scalar.copy, grouped[0], result[:, 0:2, halves[0]], 0)
-        terms = [gated(last, d, slice(0, V)) for d in range(D)]
-        partial = keep.tile([P, V], F32, name="partial", tag=f"sum{last - 1}")
-        for half in halves:
-            nc.vector.tensor_tensor(partial[:, half], terms[0][:, half], terms[1][:, half], ADD)
-        for half in halves:
-            nc.vector.tensor_tensor(result[:, last, half], partial[:, half], terms[2][:, half], ADD)
-            nc.sync.dma_start(out_rows[:, last, half], result[:, last, half])
-        place_pair(nc.scalar.copy, grouped[0], result[:, 2:4, halves[0]], 1)
 
+        def late_term(d, cols, tag):
+            term = keep.tile([P, cols.stop - cols.start], F32, name=f"late{d}_{cols.start}", tag=tag)
+            offsets = pos_t[d][:, cols.start // 16 : cols.stop // 16]
+            nc.vector.tensor_tensor(term[:], y_t[last][:].indirect(offsets), gate_t[d][:, cols], MULT)
+            return term
+
+        terms = [late_term(d, slice(0, V), f"late{d}") for d in range(D - 1)]
+        partial = [keep.tile([P, V // 2], F32, name=f"partial{a}", tag=f"sum{last - 1}_{a}") for a in range(2)]
         codes, scale = mx_tiles("out", V)
         out_words = out_1[0].rearrange("p n t -> p (n t)").bitcast(I32)
+        blocks = [slice(2 * P, 3 * P), slice(3 * P, V)]
 
-        def hand_on(a):
-            quantize_into(codes[:, halves[a]], scale[:, halves[a]], grouped[a][:].rearrange("p c t -> p (c t)"))
-            nc.sync.dma_start(out_words[:, halves[a]], codes[:, halves[a]].bitcast(I32))
+        def final_sum(term, cols):
+            a, start = divmod(cols.start, V // 2)
+            nc.vector.tensor_tensor(
+                result[:, last, cols], partial[a][:, start : start + cols.stop - cols.start], term[:], ADD
+            )
 
-        place_pair(nc.vector.tensor_copy, grouped[1], result[:, 2:4, halves[1]], 1)
-        hand_on(1)
-        hand_on(0)
+        def grouped_part(cols):
+            a, start = divmod(cols.start, V // 2)
+            return grouped[a][:, start : start + cols.stop - cols.start, :]
+
+        def quantize_out(cols):
+            quantize_into(codes[:, cols], scale[:, cols], grouped_part(cols).rearrange("p c t -> p (c t)"))
+
+        term = late_term(D - 1, halves[0], "late2")
+        for a, half in enumerate(halves):
+            nc.vector.tensor_tensor(partial[a][:], terms[0][:, half], terms[1][:, half], ADD)
+        final_sum(term, halves[0])
+        nc.sync.dma_start(out_rows[:, last, halves[0]], result[:, last, halves[0]])
+        place_pair(nc.scalar.copy, grouped[0], result[:, 2:4, halves[0]], 1)
+        block_terms = [late_term(D - 1, cols, tag) for cols, tag in zip(blocks, ("late0", "late2"))]
+        for term, cols in zip(block_terms, blocks):
+            final_sum(term, cols)
+        nc.sync.dma_start(out_rows[:, last, halves[1]], result[:, last, halves[1]])
+        place_pair(nc.scalar.copy, grouped_part(blocks[0]), result[:, 2:4, blocks[0]], 1)
+        quantize_out(halves[0])
+        nc.sync.dma_start(out_words[:, halves[0]], codes[:, halves[0]].bitcast(I32))
+        place_pair(nc.vector.tensor_copy, grouped_part(blocks[1]), result[:, 2:4, blocks[1]], 1)
+        for cols in blocks:
+            quantize_out(cols)
+        nc.sync.dma_start(out_words[:, halves[1]], codes[:, halves[1]].bitcast(I32))
         for q in range(4):
             queue = nc.scalar if q % 2 == 0 else nc.sync
             queue.dma_start(out_2[0, 4 * q : 4 * q + 4, :].bitcast(I32), scale[32 * q : 32 * q + 4, :].bitcast(I32))

@@ -216,19 +216,19 @@ def tile_picked_devox_none_po_kernel(
         for h in range(2):
             if h == 1:
                 nc.vector.tensor_copy(windows[1][:].indirect(cell_t[:]), h_t[1][:])
-            for a in range(2):
+            for a in (1, 0):
                 cells = slice(a * HALF, (a + 1) * HALF)
                 turned = bank(2 + 2 * h + a)
                 add_turned(turned, emb_t[h][:, cells], True, False)
                 add_turned(turned, windows[h][:, cells], False, True)
                 nc.scalar.copy(z_turned[a][:, :, h, :], turned[:].rearrange("p (b q) -> p b q", q=P))
-        for a in range(2):
+        for a in (1, 0):
             back = bank(6 + a)
             words = z_turned[a][:].rearrange("p b h q -> p (b h q)").bitcast(F32)
             for b in range(BLOCKS):
                 cols = slice(b * P, (b + 1) * P)
                 nc.tensor.transpose(back[:, cols], words[:, cols], identity[:])
-            for c in (2 * a + 1, 2 * a):
+            for c in ((0, 1), (3, 2))[a]:
                 part = back[:, (c % 2) * QUARTER : (c % 2 + 1) * QUARTER]
                 nc.scalar.copy(
                     z_grouped[c].bitcast(F32).rearrange("p (c u) -> p c u", u=2),

@@ -104,6 +104,9 @@ def tile_picked_devox_none_po_kernel(
         nc.sync.dma_start(x_word_table[:].bitcast(I32), x_words[0].rearrange("p n t -> p (n t)").bitcast(I32))
         nc.sync.dma_start(w1_raw[1][:], w1_rows[:, :, H // 2 : H])
         cell_t = load_list("cell", cell)
+        w2_raw = keep.tile([P, 2 * H], U8, name="w2_raw", align_bytes=64)
+        nc.sync.dma_start(w2_raw[:].bitcast(I32), w2_words[0].bitcast(I32))
+        load_scale_rows(w2_scale_raw, w2_scales)
 
         emb_pairs = emb.rearrange("(h m t) c -> h t m c", h=2, t=PACK)
         emb_rows = emb.rearrange("(p t) c -> p t c", t=PACK)
@@ -115,9 +118,6 @@ def tile_picked_devox_none_po_kernel(
                 nc.sync.dma_start(emb_t[h][e:P:2, :], emb_pairs[h, e])
             if h == 0:
                 nc.sync.dma_start(emb_head[:], emb_rows[:, 3, 0 : 3 * QUARTER])
-        w2_raw = keep.tile([P, 2 * H], U8, name="w2_raw", align_bytes=64)
-        nc.sync.dma_start(w2_raw[:].bitcast(I32), w2_words[0].bitcast(I32))
-        load_scale_rows(w2_scale_raw, w2_scales)
         nc.sync.dma_start(emb_t[2][:], emb_rows[:, 2, :])
         nc.sync.dma_start(emb_tail[:], emb_rows[:, 3, 3 * QUARTER : U])
         pos_t = [load_list(f"pos{d + 1}", src) for d, src in enumerate((pos1, pos2, pos3))]
@@ -355,12 +355,11 @@ def tile_picked_devox_none_po_kernel(
         for a, half in enumerate(halves):
             nc.vector.tensor_tensor(partial[a][:], terms[0][:, half], terms[1][:, half], ADD)
         final_sum(term, halves[0])
-        nc.sync.dma_start(out_rows[:, last, halves[0]], result[:, last, halves[0]])
         place_pair(nc.scalar.copy, grouped[0], result[:, 2:4, halves[0]], 1)
         block_terms = [late_term(D - 1, cols, tag) for cols, tag in zip(blocks, ("late0", "late2"))]
         for term, cols in zip(block_terms, blocks):
             final_sum(term, cols)
-        nc.sync.dma_start(out_rows[:, last, halves[1]], result[:, last, halves[1]])
+        nc.sync.dma_start(out_rows[:, last, :], result[:, last, :])
         place_pair(nc.scalar.copy, grouped_part(blocks[0]), result[:, 2:4, blocks[0]], 1)
         quantize_out(halves[0])
         nc.sync.dma_start(out_words[:, halves[0]], codes[:, halves[0]].bitcast(I32))

@@ -97,8 +97,8 @@ def tile_picked_devox_none_po_kernel(
 
         w1_rows = w1.rearrange("(p j) c -> p j c", j=PACK)
         w1_raw = [keep.tile([P, PACK, H // 2], F32, name=f"w1_raw{h}", tag=f"w1_raw{h}") for h in range(2)]
-        offs_t = load_list("offs", offs)
         nc.sync.dma_start(w1_raw[0][:], w1_rows[:, :, 0 : H // 2])
+        offs_t = load_list("offs", offs)
         load_scale_rows(x_scale_table, x_scales)
         x_word_table = keep.tile([P, T], U32, name="x_word_table", align_bytes=64)
         nc.sync.dma_start(x_word_table[:].bitcast(I32), x_words[0].rearrange("p n t -> p (n t)").bitcast(I32))
@@ -332,8 +332,7 @@ def tile_picked_devox_none_po_kernel(
             nc.vector.tensor_tensor(term[:], y_t[last][:].indirect(offsets), gate_t[d][:, cols], MULT)
             return term
 
-        terms = [late_term(d, slice(0, V), f"late{d}") for d in range(D - 1)]
-        partial = [keep.tile([P, V // 2], F32, name=f"partial{a}", tag=f"sum{last - 1}_{a}") for a in range(2)]
+        first_term = late_term(0, slice(0, V), "late0")
         codes, scale = mx_tiles("out", V)
         out_words = out_1[0].rearrange("p n t -> p (n t)").bitcast(I32)
         blocks = [slice(2 * P, 3 * P), slice(3 * P, V)]
@@ -351,15 +350,24 @@ def tile_picked_devox_none_po_kernel(
         def quantize_out(cols):
             quantize_into(codes[:, cols], scale[:, cols], grouped_part(cols).rearrange("p c t -> p (c t)"))
 
-        term = late_term(D - 1, halves[0], "late2")
-        for a, half in enumerate(halves):
-            nc.vector.tensor_tensor(partial[a][:], terms[0][:, half], terms[1][:, half], ADD)
-        final_sum(term, halves[0])
+        def partial_sum(a, term, tag):
+            partial.append(keep.tile([P, V // 2], F32, name=f"partial{a}", tag=tag))
+            nc.vector.tensor_tensor(partial[a][:], first_term[:, halves[a]], term[:], ADD)
+
+        partial = []
+        second_low = late_term(1, halves[0], "late1")
+        third_low = late_term(2, halves[0], "late2")
+        partial_sum(0, second_low, "sum2_0")
+        second_high = late_term(1, halves[1], "sum2_1")
+        final_sum(third_low, halves[0])
+        nc.sync.dma_start(out_rows[:, last, halves[0]], result[:, last, halves[0]])
         place_pair(nc.scalar.copy, grouped[0], result[:, 2:4, halves[0]], 1)
-        block_terms = [late_term(D - 1, cols, tag) for cols, tag in zip(blocks, ("late0", "late2"))]
+        block_terms = [late_term(2, blocks[0], "late1")]
+        partial_sum(1, second_high, "partial1")
+        block_terms.append(late_term(2, blocks[1], "late2"))
         for term, cols in zip(block_terms, blocks):
             final_sum(term, cols)
-        nc.sync.dma_start(out_rows[:, last, :], result[:, last, :])
+        nc.sync.dma_start(out_rows[:, last, halves[1]], result[:, last, halves[1]])
         place_pair(nc.scalar.copy, grouped_part(blocks[0]), result[:, 2:4, blocks[0]], 1)
         quantize_out(halves[0])
         nc.sync.dma_start(out_words[:, halves[0]], codes[:, halves[0]].bitcast(I32))

@@ -22,7 +22,6 @@ P = 128
 PACK = 4
 T, S, V, H, U, D = 2048, 512, 512, 512, 1024, 3
 HALF = 512
-BLOCKS = HALF // P
 QUARTER = 256
 
 
@@ -33,7 +32,6 @@ def tile_picked_devox_none_po_kernel(
     with ExitStack() as ctx:
         lists = ctx.enter_context(tc.tile_pool(name="lists", bufs=1))
         keep = ctx.enter_context(tc.tile_pool(name="keep", bufs=1))
-        ring = ctx.enter_context(tc.tile_pool(name="ring", bufs=2))
         psum = ctx.enter_context(tc.psum_pool(name="psum", bufs=1))
 
         def bank(k, columns=HALF):
@@ -43,6 +41,9 @@ def tile_picked_devox_none_po_kernel(
             tile = lists.tile([P, S // 16], U16, name=name)
             nc.sync.dma_start(tile[:], src)
             return tile
+
+        def entries(tile, cols):
+            return tile[:, cols.start // 16 : cols.stop // 16]
 
         def load_scale_rows(tile, rows):
             for q in range(4):
@@ -56,24 +57,8 @@ def tile_picked_devox_none_po_kernel(
         def quantize_into(codes, scale, grouped):
             nc.vector.quantize_mx(out=codes.bitcast(FP8X4), scales=scale, in_=grouped)
 
-        def quantize(name, grouped):
-            codes, scale = mx_tiles(name, grouped.shape[1] // PACK)
-            quantize_into(codes[:], scale[:], grouped)
-            return codes, scale
-
-        def add_turned(target, source, first, last):
-            for b in range(BLOCKS):
-                cols = slice(b * P, (b + 1) * P)
-                nc.tensor.matmul(
-                    target[:, cols],
-                    source[:, cols],
-                    identity[:],
-                    start=(first and b == 0),
-                    stop=(last and b == BLOCKS - 1),
-                    is_transpose=True,
-                )
-
-        def turn_all(target, source, blocks, first, last):
+        def turn(target, source, first, last):
+            blocks = source.shape[1] // P
             for b in range(blocks):
                 cols = slice(b * P, (b + 1) * P)
                 nc.tensor.matmul(
@@ -90,37 +75,35 @@ def tile_picked_devox_none_po_kernel(
 
         x_scale_table = keep.tile([P, T], U8, name="x_scale_table", align_bytes=64)
         nc.gpsimd.memset(x_scale_table[:].bitcast(I32), 0)
-        w2_scale_raw = keep.tile([P, H], U8, name="w2_scale_raw", align_bytes=64)
+        w2_scale_raw = keep.tile([P, H], U8, name="w2_scale_raw", tag="z_rows1", align_bytes=64)
         nc.gpsimd.memset(w2_scale_raw[:].bitcast(I32), 0)
         identity = keep.tile([P, P], F32, name="identity")
         make_identity(nc, identity[:])
 
         w1_rows = w1.rearrange("(p j) c -> p j c", j=PACK)
-        w1_raw = [keep.tile([P, PACK, H // 2], F32, name=f"w1_raw{h}", tag=f"w1_raw{h}") for h in range(2)]
+        w1_raw = [keep.tile([P, PACK, H // 2], F32, name=f"w1_raw{h}") for h in range(2)]
         nc.sync.dma_start(w1_raw[0][:], w1_rows[:, :, 0 : H // 2])
         offs_t = load_list("offs", offs)
         load_scale_rows(x_scale_table, x_scales)
+        nc.sync.dma_start(w1_raw[1][:], w1_rows[:, :, H // 2 : H])
         x_word_table = keep.tile([P, T], U32, name="x_word_table", align_bytes=64)
         nc.sync.dma_start(x_word_table[:].bitcast(I32), x_words[0].rearrange("p n t -> p (n t)").bitcast(I32))
-        nc.sync.dma_start(w1_raw[1][:], w1_rows[:, :, H // 2 : H])
         cell_t = load_list("cell", cell)
-        w2_raw = keep.tile([P, 2 * H], U8, name="w2_raw", align_bytes=64)
+        emb_rows = emb.rearrange("(p t) c -> p t c", t=PACK)
+        emb_t = [keep.tile([P, U if t < 3 else HALF], F32, name=f"emb{t}") for t in range(PACK)]
+        w2_raw = keep.tile([P, 2 * H], U8, name="w2_raw", tag="z_rows0", align_bytes=64)
         nc.sync.dma_start(w2_raw[:].bitcast(I32), w2_words[0].bitcast(I32))
         load_scale_rows(w2_scale_raw, w2_scales)
-
-        emb_pairs = emb.rearrange("(h m t) c -> h t m c", h=2, t=PACK)
-        emb_rows = emb.rearrange("(p t) c -> p t c", t=PACK)
-        emb_t = [keep.tile([P, U], F32, name=f"emb{t}") for t in range(PACK - 1)]
-        emb_head = keep.tile([P, 3 * QUARTER], F32, name="emb_head")
-        emb_tail = keep.tile([P, QUARTER], F32, name="emb_tail")
-        for h in range(2):
-            for e in range(2):
-                nc.sync.dma_start(emb_t[h][e:P:2, :], emb_pairs[h, e])
-            if h == 0:
-                nc.sync.dma_start(emb_head[:], emb_rows[:, 3, 0 : 3 * QUARTER])
-        nc.sync.dma_start(emb_t[2][:], emb_rows[:, 2, :])
-        nc.sync.dma_start(emb_tail[:], emb_rows[:, 3, 3 * QUARTER : U])
+        for t in (0, 2, 1):
+            nc.sync.dma_start(emb_t[t][:], emb_rows[:, t, :])
+        nc.sync.dma_start(emb_t[3][:], emb_rows[:, 3, 0:HALF])
+        gate_rows = keep.tile([P, P], F32, name="gate_rows")
+        nc.gpsimd.memset(gate_rows[:], 0.0)
+        for d in range(D):
+            nc.sync.dma_start(gate_rows[4 * d : 4 * d + 4, :], gate[d, 0, :].rearrange("(b c) -> b c", c=P))
         pos_t = [load_list(f"pos{d + 1}", src) for d, src in enumerate((pos1, pos2, pos3))]
+        emb_last = keep.tile([P, HALF], F32, name="emb_last")
+        nc.sync.dma_start(emb_last[:], emb_rows[:, 3, HALF:U])
         gate_t = []
         for d in range(D):
             tile = keep.tile([P, V], F32, name=f"gate{d}")
@@ -128,143 +111,140 @@ def tile_picked_devox_none_po_kernel(
             gate_t.append(tile)
 
         windows = []
-        for w in range(3):
-            tile = keep.tile([P, U], F32, name=f"window{w}")
-            nc.vector.memset(tile[:], 0.0)
+        for t in range(PACK):
+            tile = keep.tile([P, U], F32, name=f"window{t}")
+            (nc.vector if t < 2 else nc.gpsimd).memset(tile[:], 0.0)
             windows.append(tile)
-
 
         x_scale = keep.tile([P, S], U8, name="x_scale", align_bytes=64)
         nc.vector.tensor_copy(x_scale[:], x_scale_table[:].indirect(offs_t[:]))
 
-        w1_low = [keep.tile([P, P // 2, 2, PACK], BF16, name=f"w1_low{h}", tag=f"w1_low{h}", align_bytes=64) for h in range(2)]
-        w1_high = keep.tile([P, 2, P, PACK], BF16, name="w1_high", tag="w1_high", align_bytes=64)
-
-        def round_low(copy, h):
-            view = w1_raw[h][:].rearrange("p j (m t) -> p m j t", t=PACK)
-            copy(w1_low[h][:].rearrange("p m e j -> p m j e"), view[:, :, :, 0:2])
-
-        def round_high(h):
-            view = w1_raw[h][:].rearrange("p j (m t) -> p m j t", t=PACK)
+        w1_grouped = keep.tile([P, PACK, P, PACK], BF16, name="w1_grouped", align_bytes=64)
+        for h, copy in enumerate((nc.scalar.copy, nc.vector.tensor_copy)):
             rows = slice(h * (P // 2), (h + 1) * (P // 2))
-            nc.scalar.activation(w1_high[:, :, rows, :].rearrange("p t m j -> p m j t"), view[:, :, :, 2:4], COPY)
+            copy(
+                w1_grouped[:, :, rows, :].rearrange("p t m j -> p m t j"),
+                w1_raw[h][:].rearrange("p j (m t) -> p m t j", t=PACK),
+            )
+        w1_codes, w1_scale = mx_tiles("w1", H)
+        quantize_into(w1_codes[:], w1_scale[:], w1_grouped[:].rearrange("p t m j -> p (t m j)"))
 
-        round_low(nc.scalar.copy, 0)
-        round_high(0)
-        w1_mx = [quantize("w1_low0", w1_low[0][:].rearrange("p m e j -> p (m e j)"))]
+        head, rest = slice(0, P), slice(P, S)
+        x_head = keep.tile([P, P], U32, name="x_head", align_bytes=64)
+        nc.vector.tensor_copy(x_head[:], x_word_table[:].indirect(entries(offs_t, head)))
+        x_rest = keep.tile([P, S - P], U32, name="x_rest", align_bytes=64)
+        nc.vector.tensor_copy(x_rest[:], x_word_table[:].indirect(entries(offs_t, rest)))
 
-        x_codes = keep.tile([P, S], U32, name="x_codes", align_bytes=64)
-        for a in range(2):
-            nc.vector.tensor_copy(
-                x_codes[:, a * (S // 2) : (a + 1) * (S // 2)], x_word_table[:].indirect(offs_t[:, 16 * a : 16 * a + 16])
+        def x_codes(points):
+            if points.start < P:
+                return x_head[:, points]
+            return x_rest[:, points.start - P : points.stop - P]
+
+        def first_layer(acc, t, points):
+            cols = slice(t * P, (t + 1) * P)
+            nc.tensor.matmul_mx(
+                out=acc,
+                lhsT=w1_codes[:, cols].bitcast(FP8X4),
+                lhsT_scale=w1_scale[:, cols],
+                rhs=x_codes(points).bitcast(FP8X4),
+                rhs_scale=x_scale[:, points],
+                start=True,
+                stop=True,
             )
 
-        def first_layer(hidden, codes, scale, pieces, k):
-            start = pieces[0].start
-            acc = bank(k, pieces[-1].stop - start)
-            for points in pieces:
-                nc.tensor.matmul_mx(
-                    out=acc[:, points.start - start : points.stop - start],
-                    lhsT=codes.bitcast(FP8X4),
-                    lhsT_scale=scale,
-                    rhs=x_codes[:, points].bitcast(FP8X4),
-                    rhs_scale=x_scale[:, points],
-                    start=True,
-                    stop=True,
-                )
-            nc.scalar.activation(hidden[:], acc[:], RELU)
+        def scatter(t, points, values):
+            target = windows[t][:].indirect(entries(cell_t, points))
+            if t % 2 == 0:
+                nc.vector.tensor_copy(target, values)
+            else:
+                nc.scalar.activation(target, values, COPY)
 
-        round_low(nc.vector.tensor_copy, 1)
-        first = keep.tile([P, P], F32, name="h0_first")
-        first_layer(first, w1_mx[0][0][:], w1_mx[0][1][:], [slice(0, P)], 0)
-        nc.vector.tensor_copy(windows[0][:].indirect(cell_t[:, 0:8]), first[:])
-        low_codes, low_scale = quantize("w1_low1", w1_low[1][:].rearrange("p m e j -> p (m e j)"))
-        round_high(1)
-        high_codes, high_scale = quantize("w1_high", w1_high[:].rearrange("p t m j -> p (t m j)"))
-        second = keep.tile([P, S - P], F32, name="h0_second", tag="w1_raw1")
-        first_layer(second, w1_mx[0][0][:], w1_mx[0][1][:], [slice(P, 2 * P), slice(2 * P, S)], 1)
-        nc.vector.tensor_copy(windows[0][:].indirect(cell_t[:, 8:32]), second[:])
-        h_t = {t: keep.tile([P, S], F32, name=f"h{t}") for t in range(1, PACK)}
-        first_layer(h_t[1], low_codes[:], low_scale[:], [slice(0, S)], 0)
-        for t in range(2, PACK):
-            cols = slice((t - 2) * P, (t - 1) * P)
-            first_layer(h_t[t], high_codes[:, cols], high_scale[:, cols], [slice(0, S)], (t + 1) % 2)
+        acc = bank(0, 2 * P)
+        for t in range(2):
+            first_layer(acc[:, t * P : (t + 1) * P], t, head)
+        h_head = keep.tile([P, 2 * P], F32, name="h_head")
+        nc.scalar.activation(h_head[:], acc[:], RELU)
+        for t in range(2):
+            scatter(t, head, h_head[:, t * P : (t + 1) * P])
+        pieces = (head, slice(P, 2 * P), slice(2 * P, S))
+        h_t = {}
+        for t in (0, 2, 3, 1):
+            first = P if t < 2 else 0
+            acc = bank(1 + t, S - first)
+            for points in pieces[first // P :]:
+                first_layer(acc[:, points.start - first : points.stop - first], t, points)
+            h_t[t] = keep.tile([P, S - first], F32, name=f"h{t}")
+            nc.scalar.activation(h_t[t][:], acc[:], RELU)
+        scatter(0, rest, h_t[0][:])
+        scatter(2, slice(0, S), h_t[2][:])
+        scatter(3, head, h_t[3][:, head])
+        scatter(1, rest, h_t[1][:])
+        scatter(3, rest, h_t[3][:, rest])
 
-        w2_codes = keep.tile([P, PACK, P, 2], U8, name="w2_codes", tag="w1_high", align_bytes=64)
-        nc.gpsimd.tensor_copy(
-            w2_codes[:].rearrange("p t m b -> p m t b"), w2_raw[:].rearrange("p (m t b) -> p m t b", t=PACK, b=2)
-        )
-        w2_scale = keep.tile([P, PACK, P], U8, name="w2_scale", tag="w1_low1", align_bytes=64)
-        nc.gpsimd.tensor_copy(
-            w2_scale[:].rearrange("p t m -> p m t"), w2_scale_raw[:].rearrange("p (m t) -> p m t", t=PACK)
-        )
+        w2_codes = keep.tile([P, PACK, P, 2], U8, name="w2_codes", align_bytes=64)
+        nc.gpsimd.tensor_copy(w2_codes[:], w2_raw[:].rearrange("p (m t b) -> p t m b", t=PACK, b=2))
+        w2_scale = keep.tile([P, PACK, P], U8, name="w2_scale", align_bytes=64)
+        nc.gpsimd.tensor_copy(w2_scale[:], w2_scale_raw[:].rearrange("p (m t) -> p t m", t=PACK))
 
-        emb_turned = keep.tile([P, 3 * QUARTER], F32, name="emb_turned")
-        emb_banks = []
-        for a, cells in enumerate((slice(0, HALF), slice(HALF, HALF + QUARTER))):
-            width = cells.stop - cells.start
-            turned = bank(6 + a, width)
-            turn_all(turned, emb_head[:, cells], width // P, True, True)
-            nc.scalar.copy(emb_turned[:, cells], turned[:])
-            back = bank(a, width)
-            turn_all(back, emb_turned[:, cells], width // P, True, True)
-            emb_banks.append(back)
+        gate_cols = keep.tile([P, D, V // P], F32, name="gate_cols")
+        turned = bank(3, P)
+        turn(turned, gate_rows[:], True, True)
+        nc.vector.tensor_copy(gate_cols[:].rearrange("p d b -> p (d b)"), turned[:, 0 : D * V // P])
 
-        z_tiles = [keep.tile([P, QUARTER * PACK], BF16, name=f"z_quarter{c}", align_bytes=64) for c in range(4)]
-        z_grouped = [tile[:] for tile in z_tiles]
-        z_turned = [keep.tile([P, BLOCKS, 2, P], BF16, name=f"z_turned{a}", align_bytes=64) for a in range(2)]
-        for h in range(2):
-            if h == 1:
-                nc.vector.tensor_copy(windows[1][:].indirect(cell_t[:]), h_t[1][:])
-            for a in (1, 0):
-                cells = slice(a * HALF, (a + 1) * HALF)
-                turned = bank(2 + 2 * h + a)
-                add_turned(turned, emb_t[h][:, cells], True, False)
-                add_turned(turned, windows[h][:, cells], False, True)
-                nc.scalar.copy(z_turned[a][:, :, h, :], turned[:].rearrange("p (b q) -> p b q", q=P))
-        for a in (1, 0):
-            back = bank(6 + a)
-            words = z_turned[a][:].rearrange("p b h q -> p (b h q)").bitcast(F32)
-            for b in range(BLOCKS):
-                cols = slice(b * P, (b + 1) * P)
-                nc.tensor.transpose(back[:, cols], words[:, cols], identity[:])
-            for c in ((0, 1), (3, 2))[a]:
-                part = back[:, (c % 2) * QUARTER : (c % 2 + 1) * QUARTER]
-                nc.scalar.copy(
-                    z_grouped[c].bitcast(F32).rearrange("p (c u) -> p c u", u=2),
-                    part.rearrange("p (c o) -> p c o", o=1).to_broadcast([P, QUARTER, 2]),
-                )
-
-        z_rows = keep.tile([P, 3, 2, QUARTER], BF16, name="z_rows", align_bytes=64)
-        z_slots = [z_grouped[c].rearrange("p (n t) -> p n t", t=PACK) for c in range(4)]
         quarter = [slice(c * QUARTER, (c + 1) * QUARTER) for c in range(4)]
-        nc.vector.tensor_copy(windows[2][:].indirect(cell_t[:]), h_t[2][:])
-        nc.vector.tensor_copy(windows[0][:].indirect(cell_t[:]), h_t[3][:])
-        nc.gpsimd.tensor_tensor(
-            z_rows[:, :, 0, :],
-            windows[2][:, 0 : 3 * QUARTER].rearrange("p (c n) -> p c n", c=3),
-            emb_t[2][:, 0 : 3 * QUARTER].rearrange("p (c n) -> p c n", c=3),
-            ADD,
-        )
-        nc.gpsimd.tensor_tensor(z_slots[3][:, :, 2], windows[2][:, quarter[3]], emb_t[2][:, quarter[3]], ADD)
-        nc.gpsimd.tensor_tensor(z_slots[3][:, :, 3], windows[0][:, quarter[3]], emb_tail[:], ADD)
-        for c in (0, 2, 1):
-            nc.vector.tensor_tensor(
-                z_rows[:, c, 1, :], windows[0][:, quarter[c]], emb_banks[c // 2][:, quarter[c % 2]], ADD
-            )
-        for c in range(3):
-            place_pair(nc.scalar.copy if c < 2 else nc.vector.tensor_copy, z_slots[c], z_rows[:, c, :, :], 1)
         z_codes, z_scale = mx_tiles("z", U)
-        for c in (2, 0, 3):
-            quantize_into(z_codes[:, quarter[c]], z_scale[:, quarter[c]], z_grouped[c])
-        for a in range(2):
-            cells = slice(QUARTER + a * P, QUARTER + (a + 1) * P)
-            quantize_into(z_codes[:, cells], z_scale[:, cells], z_grouped[1][:, a * HALF : (a + 1) * HALF])
 
-        out_rows = out_0.rearrange("(p t) v -> p t v", t=PACK)
-        result = keep.tile([P, PACK, V], F32, name="result")
-        grouped = [keep.tile([P, V // 2, PACK], BF16, name="out_grouped0", align_bytes=64)]
-        halves = [slice(a * (V // 2), (a + 1) * (V // 2)) for a in range(2)]
+        def turn_block(target, source, first, last):
+            nc.tensor.matmul(target, source, identity[:], start=first, stop=last, is_transpose=True)
+
+        def turned_pairs(u, banks, copy):
+            turned = [bank(k) for k in banks]
+            sources = [(tiles[2 * u + e], e) for tiles in (emb_t, windows) for e in range(2)]
+            for i, (source, e) in enumerate(sources):
+                for c in range(2):
+                    for b in range(2):
+                        cells = slice(c * QUARTER + b * P, c * QUARTER + (b + 1) * P)
+                        place = (2 * b + e) * P
+                        turn_block(turned[c][:, place : place + P], source[:, cells], i + b == 0, i + b == len(sources))
+            for c in range(2):
+                pairs[u, c] = keep.tile([P, 2, P, 2], BF16, name=f"z_pairs{u}_{c}", align_bytes=64)
+                copy(pairs[u, c][:], turned[c][:].rearrange("q (b e p) -> q b p e", b=2, e=2))
+
+        z_rows = {c: keep.tile([P, PACK, QUARTER], BF16, name=f"z_rows{c}", tag=f"z_rows{c - 2}", align_bytes=64) for c in (2, 3)}
+
+        def add_emb(engine, t, c):
+            part = emb_t[t][:, quarter[c]] if t < 3 else emb_last[:, quarter[c - 2]]
+            engine.tensor_tensor(z_rows[c][:, t, :], windows[t][:, quarter[c]], part, ADD)
+
+        for t in range(2):
+            for c in (2, 3):
+                add_emb(nc.gpsimd, t, c)
+        pairs = {}
+        turned_pairs(0, (5, 6), nc.vector.tensor_copy)
+        for t in (2, 3):
+            for c in (2, 3):
+                add_emb(nc.vector, t, c)
+        turned_pairs(1, (7, 0), nc.scalar.copy)
+        z_grouped = [keep.tile([P, QUARTER, PACK], BF16, name=f"z_grouped{c}", align_bytes=64) for c in range(4)]
+        for c in (2, 3):
+            nc.vector.tensor_copy(
+                z_grouped[c][:].rearrange("p (n i) t -> p n t i", i=4),
+                z_rows[c][:].rearrange("p t (n i) -> p n t i", i=4),
+            )
+        for c in range(2):
+            back = bank(1 + c)
+            for u in range(2):
+                words = pairs[u, c][:].rearrange("q b p e -> q b (p e)").bitcast(F32)
+                for b in range(2):
+                    place = (2 * u + b) * P
+                    nc.tensor.transpose(back[:, place : place + P], words[:, b, :], identity[:])
+            nc.scalar.copy(
+                z_grouped[c][:].rearrange("p n t -> p (n t)").bitcast(F32).rearrange("p (n u) -> p n u", u=2),
+                back[:].rearrange("p (u n) -> p n u", u=2),
+            )
+        order = (2, 0, 3, 1)
+        for c in order:
+            quantize_into(z_codes[:, quarter[c]], z_scale[:, quarter[c]], z_grouped[c][:].rearrange("p n t -> p (n t)"))
 
         def second_layer(acc, t, cells):
             nc.tensor.matmul_mx(
@@ -277,104 +257,86 @@ def tile_picked_devox_none_po_kernel(
                 stop=True,
             )
 
-        y_t = []
-        y_banks = {1: (4, 6), 2: (2, 4), 3: (3, 2)}
-        for t in range(PACK):
-            y = keep.tile([P, U], F32, name=f"y{t}")
-            y_t.append(y)
-            if t == 0:
-                pieces = [(2, 0, QUARTER), (0, 0, QUARTER), (3, 0, QUARTER), (1, 0, P), (1, P, QUARTER)]
-                for i, (c, lo, hi) in enumerate(pieces):
-                    acc = bank(2 + i, hi - lo)
-                    second_layer(acc[:], t, slice(c * QUARTER + lo, c * QUARTER + hi))
-                    copy = nc.vector.tensor_copy if i == len(pieces) - 2 else nc.scalar.copy
-                    copy(y[:, c * QUARTER + lo : c * QUARTER + hi], acc[:])
-            else:
-                for a in range(2):
-                    acc = bank(y_banks[t][a])
-                    second_layer(acc[:], t, slice(a * HALF, (a + 1) * HALF))
-                    nc.scalar.copy(y[:, a * HALF : (a + 1) * HALF], acc[:])
+        y_t = [keep.tile([P, U], F32, name=f"y{t}") for t in range(PACK)]
+        for i, cells in enumerate([quarter[c] for c in order]):
+            acc = bank(3 + i, cells.stop - cells.start)
+            second_layer(acc[:], 0, cells)
+            copy = nc.vector.tensor_copy if i == 3 else nc.scalar.copy
+            copy(y_t[0][:, cells], acc[:])
+
+        def later_y(t):
+            for a in range(2):
+                acc = bank(3 + 2 * a)
+                second_layer(acc[:], t, slice(a * HALF, (a + 1) * HALF))
+                nc.scalar.copy(y_t[t][:, a * HALF : (a + 1) * HALF], acc[:])
+
+        out_rows = out_0.rearrange("(p t) v -> p t v", t=PACK)
+        result = keep.tile([P, PACK, V], F32, name="result")
+        halves = [slice(a * (V // 2), (a + 1) * (V // 2)) for a in range(2)]
 
         def gated(t, d, cols):
-            if (t, d) == (2, D - 1):
-                term = keep.tile([P, V], F32, name="held_term", tag="held_term", align_bytes=64)
-            else:
-                term = ring.tile([P, cols.stop - cols.start], F32, name=f"term{d}")
-            offsets = pos_t[d][:, cols.start // 16 : cols.stop // 16]
-            nc.vector.tensor_tensor(term[:], y_t[t][:].indirect(offsets), gate_t[d][:, cols], MULT)
+            term = keep.tile([P, cols.stop - cols.start], F32, name=f"term{t}_{d}_{cols.start}")
+            nc.vector.tensor_tensor(term[:], y_t[t][:].indirect(entries(pos_t[d], cols)), gate_t[d][:, cols], MULT)
             return term
 
-        def summed_by_transposes(t, cols):
+        def vector_sum(t, cols):
+            terms = [gated(t, d, cols) for d in range(D)]
+            partial = keep.tile([P, cols.stop - cols.start], F32, name=f"partial{t}_{cols.start}")
+            nc.vector.tensor_tensor(partial[:], terms[0][:], terms[1][:], ADD)
+            nc.vector.tensor_tensor(result[:, t, cols], partial[:], terms[2][:], ADD)
+
+        def fetch_turned(t, d, cols):
             width = cols.stop - cols.start
-            turned = bank(min(t, 1), width)
-            for d in range(D):
-                turn_all(turned, gated(t, d, cols)[:], width // P, d == 0, d == D - 1)
-            back = bank(6 + t % 2, width)
-            for a, part in enumerate(halves if t == 2 else [cols]):
-                turned_sb = keep.tile([P, part.stop - part.start], F32, name=f"turned_sb{t}_{a}", tag=f"sum{t}_{a}")
-                nc.scalar.copy(turned_sb[:], turned[:, part])
-                turn_all(back[:, part], turned_sb[:], (part.stop - part.start) // P, True, True)
-            if t == 2:
-                grouped.append(keep.tile([P, V // 2, PACK], BF16, name="out_grouped1", tag="held_term", align_bytes=64))
-                place_pair(nc.scalar.copy, grouped[1], result[:, 0:2, halves[1]], 0)
-            nc.scalar.copy(result[:, t, cols], back[:])
+            plain = keep.tile([P, width], F32, name=f"plain{t}_{d}")
+            nc.scalar.activation(plain[:], y_t[t][:].indirect(entries(pos_t[d], cols)), COPY)
+            turned = bank(d, width)
+            turn(turned, plain[:], True, True)
+            return turned
 
-        last = PACK - 1
-        for t in range(last):
-            summed_by_transposes(t, slice(0, V))
-            nc.sync.dma_start(out_rows[:, t, :], result[:, t, :])
-            if t == 1:
-                place_pair(nc.scalar.copy, grouped[0], result[:, 0:2, halves[0]], 0)
+        def gate_turned(back, turned, t, d, cols):
+            width = cols.stop - cols.start
+            weighted = keep.tile([P, width], F32, name=f"weighted{t}_{d}")
+            for b in range(width // P):
+                block = slice(b * P, (b + 1) * P)
+                k = cols.start // P + b
+                nc.scalar.activation(weighted[:, block], turned[:, block], COPY, scale=gate_cols[:, d, k : k + 1])
+            turn(back, weighted[:], d == 0, d == D - 1)
 
-        def late_term(d, cols, tag):
-            term = keep.tile([P, cols.stop - cols.start], F32, name=f"late{d}_{cols.start}", tag=tag)
-            offsets = pos_t[d][:, cols.start // 16 : cols.stop // 16]
-            nc.vector.tensor_tensor(term[:], y_t[last][:].indirect(offsets), gate_t[d][:, cols], MULT)
-            return term
+        whole = slice(0, V)
+        later_y(1)
+        vector_sum(0, halves[1])
+        turned0 = [fetch_turned(0, d, halves[0]) for d in range(D)]
+        later_y(2)
+        back = bank(4, V // 2)
+        for d in range(D):
+            gate_turned(back, turned0[d], 0, d, halves[0])
+        later_y(3)
+        nc.scalar.copy(result[:, 0, halves[0]], back[:])
+        nc.sync.dma_start(out_rows[:, 0, :], result[:, 0, :])
+        turned2 = [fetch_turned(2, 0, whole)]
+        vector_sum(1, whole)
+        nc.sync.dma_start(out_rows[:, 1, :], result[:, 1, :])
+        grouped = [keep.tile([P, V // 2, PACK], BF16, name=f"out_grouped{a}", align_bytes=64) for a in range(2)]
+        for a in range(2):
+            place_pair(nc.vector.tensor_copy, grouped[a], result[:, 0:2, halves[a]], 0)
+        back = bank(7)
+        for d in range(D):
+            if d + 1 < D:
+                turned2.append(fetch_turned(2, d + 1, whole))
+            gate_turned(back, turned2[d], 2, d, whole)
+        nc.scalar.copy(result[:, 2, :], back[:])
+        nc.sync.dma_start(out_rows[:, 2, :], result[:, 2, :])
 
-        first_term = late_term(0, slice(0, V), "late0")
         codes, scale = mx_tiles("out", V)
         out_words = out_1[0].rearrange("p n t -> p (n t)").bitcast(I32)
-        blocks = [slice(2 * P, 3 * P), slice(3 * P, V)]
-
-        def final_sum(term, cols):
-            a, start = divmod(cols.start, V // 2)
-            nc.vector.tensor_tensor(
-                result[:, last, cols], partial[a][:, start : start + cols.stop - cols.start], term[:], ADD
-            )
-
-        def grouped_part(cols):
-            a, start = divmod(cols.start, V // 2)
-            return grouped[a][:, start : start + cols.stop - cols.start, :]
-
-        def quantize_out(cols):
-            quantize_into(codes[:, cols], scale[:, cols], grouped_part(cols).rearrange("p c t -> p (c t)"))
-
-        def partial_sum(a, term, tag):
-            partial.append(keep.tile([P, V // 2], F32, name=f"partial{a}", tag=tag))
-            nc.vector.tensor_tensor(partial[a][:], first_term[:, halves[a]], term[:], ADD)
-
-        partial = []
-        second_low = late_term(1, halves[0], "late1")
-        third_low = late_term(2, halves[0], "late2")
-        partial_sum(0, second_low, "sum2_0")
-        second_high = late_term(1, halves[1], "sum2_1")
-        final_sum(third_low, halves[0])
-        nc.sync.dma_start(out_rows[:, last, halves[0]], result[:, last, halves[0]])
-        place_pair(nc.scalar.copy, grouped[0], result[:, 2:4, halves[0]], 1)
-        block_terms = [late_term(2, blocks[0], "late1")]
-        partial_sum(1, second_high, "partial1")
-        block_terms.append(late_term(2, blocks[1], "late2"))
-        for term, cols in zip(block_terms, blocks):
-            final_sum(term, cols)
-        nc.sync.dma_start(out_rows[:, last, halves[1]], result[:, last, halves[1]])
-        place_pair(nc.scalar.copy, grouped_part(blocks[0]), result[:, 2:4, blocks[0]], 1)
-        quantize_out(halves[0])
-        nc.sync.dma_start(out_words[:, halves[0]], codes[:, halves[0]].bitcast(I32))
-        place_pair(nc.vector.tensor_copy, grouped_part(blocks[1]), result[:, 2:4, blocks[1]], 1)
-        for cols in blocks:
-            quantize_out(cols)
-        nc.sync.dma_start(out_words[:, halves[1]], codes[:, halves[1]].bitcast(I32))
+        for a in range(2):
+            vector_sum(3, halves[a])
+            nc.sync.dma_start(out_rows[:, 3, halves[a]], result[:, 3, halves[a]])
+        for a in range(2):
+            place_pair((nc.scalar.copy, nc.vector.tensor_copy)[a], grouped[a], result[:, 2:4, halves[a]], 1)
+        for a in (1, 0):
+            quantize_into(codes[:, halves[a]], scale[:, halves[a]], grouped[a][:].rearrange("p c t -> p (c t)"))
+            nc.sync.dma_start(out_words[:, halves[a]], codes[:, halves[a]].bitcast(I32))
         for q in range(4):
             queue = nc.scalar if q % 2 == 0 else nc.sync
             queue.dma_start(out_2[0, 4 * q : 4 * q + 4, :].bitcast(I32), scale[32 * q : 32 * q + 4, :].bitcast(I32))

@@ -90,20 +90,19 @@ def tile_picked_devox_none_po_kernel(
         nc.sync.dma_start(x_word_table[:].bitcast(I32), x_words[0].rearrange("p n t -> p (n t)").bitcast(I32))
         cell_t = load_list("cell", cell)
         emb_rows = emb.rearrange("(p t) c -> p t c", t=PACK)
-        emb_t = [keep.tile([P, U if t < 3 else HALF], F32, name=f"emb{t}") for t in range(PACK)]
+        emb_t = [keep.tile([P, U if t < 2 else HALF], F32, name=f"emb{t}") for t in range(PACK)]
         w2_raw = keep.tile([P, 2 * H], U8, name="w2_raw", tag="z_rows0", align_bytes=64)
         nc.sync.dma_start(w2_raw[:].bitcast(I32), w2_words[0].bitcast(I32))
         load_scale_rows(w2_scale_raw, w2_scales)
-        for t in (0, 2, 1):
-            nc.sync.dma_start(emb_t[t][:], emb_rows[:, t, :])
-        nc.sync.dma_start(emb_t[3][:], emb_rows[:, 3, 0:HALF])
+        for t in (0, 2, 1, 3):
+            nc.sync.dma_start(emb_t[t][:], emb_rows[:, t, 0 : emb_t[t].shape[1]])
+        emb_upper = keep.tile([P, 2, HALF], F32, name="emb_upper")
+        nc.sync.dma_start(emb_upper[:], emb_rows[:, 2:4, HALF:U])
         gate_rows = keep.tile([P, P], F32, name="gate_rows")
         nc.gpsimd.memset(gate_rows[:], 0.0)
         for d in range(D):
             nc.sync.dma_start(gate_rows[4 * d : 4 * d + 4, :], gate[d, 0, :].rearrange("(b c) -> b c", c=P))
         pos_t = [load_list(f"pos{d + 1}", src) for d, src in enumerate((pos1, pos2, pos3))]
-        emb_last = keep.tile([P, HALF], F32, name="emb_last")
-        nc.sync.dma_start(emb_last[:], emb_rows[:, 3, HALF:U])
         gate_t = []
         for d in range(D):
             tile = keep.tile([P, V], F32, name=f"gate{d}")
@@ -213,7 +212,7 @@ def tile_picked_devox_none_po_kernel(
         z_rows = {c: keep.tile([P, PACK, QUARTER], BF16, name=f"z_rows{c}", tag=f"z_rows{c - 2}", align_bytes=64) for c in (2, 3)}
 
         def add_emb(engine, t, c):
-            part = emb_t[t][:, quarter[c]] if t < 3 else emb_last[:, quarter[c - 2]]
+            part = emb_t[t][:, quarter[c]] if t < 2 else emb_upper[:, t - 2, quarter[c - 2]]
             engine.tensor_tensor(z_rows[c][:, t, :], windows[t][:, quarter[c]], part, ADD)
 
         for t in range(2):
@@ -279,61 +278,70 @@ def tile_picked_devox_none_po_kernel(
             nc.vector.tensor_tensor(term[:], y_t[t][:].indirect(entries(pos_t[d], cols)), gate_t[d][:, cols], MULT)
             return term
 
-        def vector_sum(t, cols):
-            terms = [gated(t, d, cols) for d in range(D)]
-            partial = keep.tile([P, cols.stop - cols.start], F32, name=f"partial{t}_{cols.start}")
-            nc.vector.tensor_tensor(partial[:], terms[0][:], terms[1][:], ADD)
-            nc.vector.tensor_tensor(result[:, t, cols], partial[:], terms[2][:], ADD)
-
-        def fetch_turned(t, d, cols):
-            width = cols.stop - cols.start
-            plain = keep.tile([P, width], F32, name=f"plain{t}_{d}")
-            nc.scalar.activation(plain[:], y_t[t][:].indirect(entries(pos_t[d], cols)), COPY)
-            turned = bank(d, width)
+        def fetch_turned(t, d):
+            plain = keep.tile([P, V], F32, name=f"plain{t}_{d}", tag=f"plain{t}_{d}", align_bytes=64)
+            nc.scalar.activation(plain[:], y_t[t][:].indirect(pos_t[d][:]), COPY)
+            turned = bank(d - 1)
             turn(turned, plain[:], True, True)
             return turned
 
-        def gate_turned(back, turned, t, d, cols):
-            width = cols.stop - cols.start
-            weighted = keep.tile([P, width], F32, name=f"weighted{t}_{d}")
-            for b in range(width // P):
+        def gate_turned(back, turned, t, d):
+            weighted = keep.tile([P, V], F32, name=f"weighted{t}_{d}", tag=f"weighted{t}_{d}", align_bytes=64)
+            for b in range(V // P):
                 block = slice(b * P, (b + 1) * P)
-                k = cols.start // P + b
-                nc.scalar.activation(weighted[:, block], turned[:, block], COPY, scale=gate_cols[:, d, k : k + 1])
-            turn(back, weighted[:], d == 0, d == D - 1)
+                nc.scalar.activation(weighted[:, block], turned[:, block], COPY, scale=gate_cols[:, d, b : b + 1])
+            turn(back, weighted[:], d == 1, d == D - 1)
+
+        def finish(t, back, term):
+            nc.vector.tensor_tensor(result[:, t, :], back[:], term[:], ADD)
+            nc.sync.dma_start(out_rows[:, t, :], result[:, t, :])
 
         whole = slice(0, V)
         later_y(1)
-        vector_sum(0, halves[1])
-        turned0 = [fetch_turned(0, d, halves[0]) for d in range(D)]
+        own0 = gated(0, 0, whole)
+        turned0 = [fetch_turned(0, 1)]
         later_y(2)
-        back = bank(4, V // 2)
-        for d in range(D):
-            gate_turned(back, turned0[d], 0, d, halves[0])
+        turned0.append(fetch_turned(0, 2))
         later_y(3)
-        nc.scalar.copy(result[:, 0, halves[0]], back[:])
-        nc.sync.dma_start(out_rows[:, 0, :], result[:, 0, :])
-        turned2 = [fetch_turned(2, 0, whole)]
-        vector_sum(1, whole)
-        nc.sync.dma_start(out_rows[:, 1, :], result[:, 1, :])
-        grouped = [keep.tile([P, V // 2, PACK], BF16, name=f"out_grouped{a}", align_bytes=64) for a in range(2)]
+        terms1 = [gated(1, d, whole) for d in range(D)]
+        own2 = gated(2, 0, whole)
+        back0 = bank(4)
+        for d in (1, 2):
+            gate_turned(back0, turned0[d - 1], 0, d)
+        turned1 = bank(2)
+        for d in range(2):
+            turn(turned1, terms1[d][:], d == 0, d == 1)
+        pair1 = keep.tile([P, V], F32, name="pair1")
+        nc.scalar.copy(pair1[:], turned1[:])
+        back1 = bank(6)
+        turn(back1, pair1[:], True, True)
+        terms3 = [gated(3, d, whole) for d in range(2)]
+        finish(0, back0, own0)
+        finish(1, back1, terms1[2])
+        turned2 = [fetch_turned(2, d) for d in (1, 2)]
+        back2 = bank(7)
+        for d in (1, 2):
+            gate_turned(back2, turned2[d - 1], 2, d)
+        partial = keep.tile([P, V], F32, name="partial")
+        nc.vector.tensor_tensor(partial[:], terms3[0][:], terms3[1][:], ADD)
+        late = [gated(3, 2, halves[a]) for a in range(2)]
         for a in range(2):
-            place_pair(nc.vector.tensor_copy, grouped[a], result[:, 0:2, halves[a]], 0)
-        back = bank(7)
-        for d in range(D):
-            if d + 1 < D:
-                turned2.append(fetch_turned(2, d + 1, whole))
-            gate_turned(back, turned2[d], 2, d, whole)
-        nc.scalar.copy(result[:, 2, :], back[:])
-        nc.sync.dma_start(out_rows[:, 2, :], result[:, 2, :])
+            nc.vector.tensor_tensor(result[:, 3, halves[a]], partial[:, halves[a]], late[a][:], ADD)
+        nc.sync.dma_start(out_rows[:, 3, :], result[:, 3, :])
+        grouped = [
+            keep.tile([P, V // 2, PACK], BF16, name=f"out_grouped{a}", tag=tag, align_bytes=64)
+            for a, tag in enumerate(("weighted2_1", "plain2_2"))
+        ]
+        for a in (1, 0):
+            place_pair(nc.scalar.copy, grouped[a], result[:, 0:2, halves[a]], 0)
+        for a in (1, 0):
+            nc.vector.tensor_tensor(result[:, 2, halves[a]], back2[:, halves[a]], own2[:, halves[a]], ADD)
+            nc.sync.dma_start(out_rows[:, 2, halves[a]], result[:, 2, halves[a]])
 
         codes, scale = mx_tiles("out", V)
         out_words = out_1[0].rearrange("p n t -> p (n t)").bitcast(I32)
-        for a in range(2):
-            vector_sum(3, halves[a])
-            nc.sync.dma_start(out_rows[:, 3, halves[a]], result[:, 3, halves[a]])
-        for a in range(2):
-            place_pair((nc.scalar.copy, nc.vector.tensor_copy)[a], grouped[a], result[:, 2:4, halves[a]], 1)
+        for a in (1, 0):
+            place_pair(nc.vector.tensor_copy, grouped[a], result[:, 2:4, halves[a]], 1)
         for a in (1, 0):
             quantize_into(codes[:, halves[a]], scale[:, halves[a]], grouped[a][:].rearrange("p c t -> p (c t)"))
             nc.sync.dma_start(out_words[:, halves[a]], codes[:, halves[a]].bitcast(I32))

@@ -84,10 +84,18 @@ def tile_picked_devox_none_po_kernel(
         w1_raw = [keep.tile([P, PACK, H // 2], F32, name=f"w1_raw{h}") for h in range(2)]
         nc.sync.dma_start(w1_raw[0][:], w1_rows[:, :, 0 : H // 2])
         offs_t = load_list("offs", offs)
-        load_scale_rows(x_scale_table, x_scales)
+        nc.sync.dma_start(x_scale_table[0:P:8, :].bitcast(I32), x_scales[0].bitcast(I32))
         nc.sync.dma_start(w1_raw[1][:], w1_rows[:, :, H // 2 : H])
         x_word_table = keep.tile([P, T], U32, name="x_word_table", align_bytes=64)
         nc.sync.dma_start(x_word_table[:].bitcast(I32), x_words[0].rearrange("p n t -> p (n t)").bitcast(I32))
+        x_scale_spread = keep.tile([P, S], U8, name="x_scale_spread", align_bytes=64)
+        nc.vector.tensor_copy(x_scale_spread[:], x_scale_table[:].indirect(offs_t[:]))
+        x_scale = keep.tile([P, S], U8, name="x_scale", align_bytes=64)
+        nc.gpsimd.memset(x_scale[:].bitcast(I32), 0)
+        for q in range(4):
+            nc.sync.dma_start(
+                x_scale[32 * q : 32 * q + 4, :].bitcast(I32), x_scale_spread[32 * q : 32 * q + 32 : 8, :].bitcast(I32)
+            )
         cell_t = load_list("cell", cell)
         emb_rows = emb.rearrange("(p t) c -> p t c", t=PACK)
         emb_t = [keep.tile([P, U if t < 2 else HALF], F32, name=f"emb{t}") for t in range(PACK)]
@@ -114,9 +122,6 @@ def tile_picked_devox_none_po_kernel(
             tile = keep.tile([P, U], F32, name=f"window{t}")
             (nc.vector if t < 2 else nc.gpsimd).memset(tile[:], 0.0)
             windows.append(tile)
-
-        x_scale = keep.tile([P, S], U8, name="x_scale", align_bytes=64)
-        nc.vector.tensor_copy(x_scale[:], x_scale_table[:].indirect(offs_t[:]))
 
         w1_grouped = keep.tile([P, PACK, P, PACK], BF16, name="w1_grouped", align_bytes=64)
         for h, copy in enumerate((nc.scalar.copy, nc.vector.tensor_copy)):
@@ -158,27 +163,26 @@ def tile_picked_devox_none_po_kernel(
             else:
                 nc.scalar.activation(target, values, COPY)
 
-        acc = bank(0, 2 * P)
-        for t in range(2):
-            first_layer(acc[:, t * P : (t + 1) * P], t, head)
-        h_head = keep.tile([P, 2 * P], F32, name="h_head")
-        nc.scalar.activation(h_head[:], acc[:], RELU)
-        for t in range(2):
-            scatter(t, head, h_head[:, t * P : (t + 1) * P])
-        pieces = (head, slice(P, 2 * P), slice(2 * P, S))
-        h_t = {}
-        for t in (0, 2, 3, 1):
-            first = P if t < 2 else 0
-            acc = bank(1 + t, S - first)
-            for points in pieces[first // P :]:
-                first_layer(acc[:, points.start - first : points.stop - first], t, points)
-            h_t[t] = keep.tile([P, S - first], F32, name=f"h{t}")
-            nc.scalar.activation(h_t[t][:], acc[:], RELU)
-        scatter(0, rest, h_t[0][:])
-        scatter(2, slice(0, S), h_t[2][:])
-        scatter(3, head, h_t[3][:, head])
-        scatter(1, rest, h_t[1][:])
-        scatter(3, rest, h_t[3][:, rest])
+        h_head = []
+        for u in range(2):
+            acc = bank(u, 2 * P)
+            for e in range(2):
+                first_layer(acc[:, e * P : (e + 1) * P], 2 * u + e, head)
+            h_head.append(keep.tile([P, 2, P], F32, name=f"h_head{u}"))
+            nc.scalar.activation(h_head[u][:].rearrange("p e n -> p (e n)"), acc[:], RELU)
+        for t in range(3):
+            scatter(t, head, h_head[t // 2][:, t % 2, :])
+        h_rest = {}
+        for t, k in ((0, 2), (2, 3), (1, 4), (3, 7)):
+            acc = bank(k, S - P)
+            for points in (slice(P, 2 * P), slice(2 * P, S)):
+                first_layer(acc[:, points.start - P : points.stop - P], t, points)
+            if t == 3:
+                scatter(3, head, h_head[1][:, 1, :])
+            h_rest[t] = keep.tile([P, S - P], F32, name=f"h_rest{t}")
+            nc.scalar.activation(h_rest[t][:], acc[:], RELU)
+        for t in (0, 2, 1, 3):
+            scatter(t, rest, h_rest[t][:])
 
         w2_codes = keep.tile([P, PACK, P, 2], U8, name="w2_codes", align_bytes=64)
         nc.gpsimd.tensor_copy(w2_codes[:], w2_raw[:].rearrange("p (m t b) -> p t m b", t=PACK, b=2))
@@ -186,7 +190,7 @@ def tile_picked_devox_none_po_kernel(
         nc.gpsimd.tensor_copy(w2_scale[:], w2_scale_raw[:].rearrange("p (m t) -> p t m", t=PACK))
 
         gate_cols = keep.tile([P, D, V // P], F32, name="gate_cols")
-        turned = bank(3, P)
+        turned = bank(4, P)
         turn(turned, gate_rows[:], True, True)
         nc.vector.tensor_copy(gate_cols[:].rearrange("p d b -> p (d b)"), turned[:, 0 : D * V // P])
 
@@ -223,7 +227,7 @@ def tile_picked_devox_none_po_kernel(
         for t in (2, 3):
             for c in (2, 3):
                 add_emb(nc.vector, t, c)
-        turned_pairs(1, (7, 0), nc.scalar.copy)
+        turned_pairs(1, (0, 1), nc.scalar.copy)
         z_grouped = [keep.tile([P, QUARTER, PACK], BF16, name=f"z_grouped{c}", align_bytes=64) for c in range(4)]
         for c in (2, 3):
             nc.vector.tensor_copy(
@@ -231,7 +235,7 @@ def tile_picked_devox_none_po_kernel(
                 z_rows[c][:].rearrange("p t (n i) -> p n t i", i=4),
             )
         for c in range(2):
-            back = bank(1 + c)
+            back = bank(2 + c)
             for u in range(2):
                 words = pairs[u, c][:].rearrange("q b p e -> q b (p e)").bitcast(F32)
                 for b in range(2):
@@ -241,9 +245,10 @@ def tile_picked_devox_none_po_kernel(
                 z_grouped[c][:].rearrange("p n t -> p (n t)").bitcast(F32).rearrange("p (n u) -> p n u", u=2),
                 back[:].rearrange("p (u n) -> p n u", u=2),
             )
-        order = (2, 0, 3, 1)
-        for c in order:
-            quantize_into(z_codes[:, quarter[c]], z_scale[:, quarter[c]], z_grouped[c][:].rearrange("p n t -> p (n t)"))
+        parts = [(2, 0, QUARTER), (0, 0, QUARTER), (3, 0, QUARTER), (1, 0, P), (1, P, QUARTER)]
+        z_cells = [slice(c * QUARTER + lo, c * QUARTER + hi) for c, lo, hi in parts]
+        for (c, lo, hi), cells in zip(parts, z_cells):
+            quantize_into(z_codes[:, cells], z_scale[:, cells], z_grouped[c][:, lo:hi, :].rearrange("p n t -> p (n t)"))
 
         def second_layer(acc, t, cells):
             nc.tensor.matmul_mx(
@@ -257,15 +262,15 @@ def tile_picked_devox_none_po_kernel(
             )
 
         y_t = [keep.tile([P, U], F32, name=f"y{t}") for t in range(PACK)]
-        for i, cells in enumerate([quarter[c] for c in order]):
-            acc = bank(3 + i, cells.stop - cells.start)
+        for i, cells in enumerate(z_cells):
+            acc = bank((4, 5, 7, 6, 0)[i], cells.stop - cells.start)
             second_layer(acc[:], 0, cells)
-            copy = nc.vector.tensor_copy if i == 3 else nc.scalar.copy
+            copy = nc.vector.tensor_copy if i >= 3 else nc.scalar.copy
             copy(y_t[0][:, cells], acc[:])
 
         def later_y(t):
             for a in range(2):
-                acc = bank(3 + 2 * a)
+                acc = bank((4, 1 if t == 1 else 7)[a])
                 second_layer(acc[:], t, slice(a * HALF, (a + 1) * HALF))
                 nc.scalar.copy(y_t[t][:, a * HALF : (a + 1) * HALF], acc[:])
 
@@ -305,7 +310,7 @@ def tile_picked_devox_none_po_kernel(
         later_y(3)
         terms1 = [gated(1, d, whole) for d in range(D)]
         own2 = gated(2, 0, whole)
-        back0 = bank(4)
+        back0 = bank(5)
         for d in (1, 2):
             gate_turned(back0, turned0[d - 1], 0, d)
         turned1 = bank(2)
@@ -319,7 +324,7 @@ def tile_picked_devox_none_po_kernel(
         finish(0, back0, own0)
         finish(1, back1, terms1[2])
         turned2 = [fetch_turned(2, d) for d in (1, 2)]
-        back2 = bank(7)
+        back2 = bank(3)
         for d in (1, 2):
             gate_turned(back2, turned2[d - 1], 2, d)
         partial = keep.tile([P, V], F32, name="partial")
@@ -330,18 +335,18 @@ def tile_picked_devox_none_po_kernel(
         nc.sync.dma_start(out_rows[:, 3, :], result[:, 3, :])
         grouped = [
             keep.tile([P, V // 2, PACK], BF16, name=f"out_grouped{a}", tag=tag, align_bytes=64)
-            for a, tag in enumerate(("weighted2_1", "plain2_2"))
+            for a, tag in enumerate(("plain2_2", "weighted2_1"))
         ]
-        for a in (1, 0):
+        for a in range(2):
             place_pair(nc.scalar.copy, grouped[a], result[:, 0:2, halves[a]], 0)
-        for a in (1, 0):
+        for a in range(2):
             nc.vector.tensor_tensor(result[:, 2, halves[a]], back2[:, halves[a]], own2[:, halves[a]], ADD)
             nc.sync.dma_start(out_rows[:, 2, halves[a]], result[:, 2, halves[a]])
 
         codes, scale = mx_tiles("out", V)
         out_words = out_1[0].rearrange("p n t -> p (n t)").bitcast(I32)
-        for a in (1, 0):
-            place_pair(nc.vector.tensor_copy, grouped[a], result[:, 2:4, halves[a]], 1)
+        for a in range(2):
+            place_pair((nc.scalar.copy, nc.vector.tensor_copy)[a], grouped[a], result[:, 2:4, halves[a]], 1)
         for a in (1, 0):
             quantize_into(codes[:, halves[a]], scale[:, halves[a]], grouped[a][:].rearrange("p c t -> p (c t)"))
             nc.sync.dma_start(out_words[:, halves[a]], codes[:, halves[a]].bitcast(I32))

@@ -241,10 +241,11 @@ def tile_picked_devox_none_po_kernel(
                 for b in range(2):
                     place = (2 * u + b) * P
                     nc.tensor.transpose(back[:, place : place + P], words[:, b, :], identity[:])
-            nc.scalar.copy(
-                z_grouped[c][:].rearrange("p n t -> p (n t)").bitcast(F32).rearrange("p (n u) -> p n u", u=2),
-                back[:].rearrange("p (u n) -> p n u", u=2),
-            )
+            for cells in ([slice(0, QUARTER)], [slice(0, P), slice(P, QUARTER)])[c]:
+                nc.scalar.copy(
+                    z_grouped[c][:, cells, :].rearrange("p n t -> p (n t)").bitcast(F32).rearrange("p (n u) -> p n u", u=2),
+                    back[:].rearrange("p (u n) -> p n u", u=2)[:, cells, :],
+                )
         parts = [(2, 0, QUARTER), (0, 0, QUARTER), (3, 0, QUARTER), (1, 0, P), (1, P, QUARTER)]
         z_cells = [slice(c * QUARTER + lo, c * QUARTER + hi) for c, lo, hi in parts]
         for (c, lo, hi), cells in zip(parts, z_cells):
@@ -314,16 +315,18 @@ def tile_picked_devox_none_po_kernel(
         for d in (1, 2):
             gate_turned(back0, turned0[d - 1], 0, d)
         turned1 = bank(2)
-        for d in range(2):
-            turn(turned1, terms1[d][:], d == 0, d == 1)
+        for d in range(D):
+            turn(turned1, terms1[d][:], d == 0, d == D - 1)
         pair1 = keep.tile([P, V], F32, name="pair1")
         nc.scalar.copy(pair1[:], turned1[:])
         back1 = bank(6)
         turn(back1, pair1[:], True, True)
         terms3 = [gated(3, d, whole) for d in range(2)]
         finish(0, back0, own0)
-        finish(1, back1, terms1[2])
-        turned2 = [fetch_turned(2, d) for d in (1, 2)]
+        turned2 = [fetch_turned(2, 1)]
+        nc.scalar.copy(result[:, 1, :], back1[:])
+        nc.sync.dma_start(out_rows[:, 1, :], result[:, 1, :])
+        turned2.append(fetch_turned(2, 2))
         back2 = bank(3)
         for d in (1, 2):
             gate_turned(back2, turned2[d - 1], 2, d)
@@ -346,8 +349,8 @@ def tile_picked_devox_none_po_kernel(
         codes, scale = mx_tiles("out", V)
         out_words = out_1[0].rearrange("p n t -> p (n t)").bitcast(I32)
         for a in range(2):
-            place_pair((nc.scalar.copy, nc.vector.tensor_copy)[a], grouped[a], result[:, 2:4, halves[a]], 1)
-        for a in (1, 0):
+            place_pair(nc.vector.tensor_copy, grouped[a], result[:, 2:4, halves[a]], 1)
+        for a in range(2):
             quantize_into(codes[:, halves[a]], scale[:, halves[a]], grouped[a][:].rearrange("p c t -> p (c t)"))
             nc.sync.dma_start(out_words[:, halves[a]], codes[:, halves[a]].bitcast(I32))
         for q in range(4):

@@ -108,8 +108,8 @@ def tile_picked_devox_none_po_kernel(
         nc.sync.dma_start(emb_upper[:], emb_rows[:, 2:4, HALF:U])
         gate_rows = keep.tile([P, P], F32, name="gate_rows")
         nc.gpsimd.memset(gate_rows[:], 0.0)
-        for d in range(D):
-            nc.sync.dma_start(gate_rows[4 * d : 4 * d + 4, :], gate[d, 0, :].rearrange("(b c) -> b c", c=P))
+        for d in (1, 2):
+            nc.sync.dma_start(gate_rows[4 * d - 4 : 4 * d, :], gate[d, 0, :].rearrange("(b c) -> b c", c=P))
         pos_t = [load_list(f"pos{d + 1}", src) for d, src in enumerate((pos1, pos2, pos3))]
         gate_t = []
         for d in range(D):
@@ -180,7 +180,10 @@ def tile_picked_devox_none_po_kernel(
             if t == 3:
                 scatter(3, head, h_head[1][:, 1, :])
             h_rest[t] = keep.tile([P, S - P], F32, name=f"h_rest{t}")
-            nc.scalar.activation(h_rest[t][:], acc[:], RELU)
+            if t == 2:
+                nc.vector.tensor_scalar_max(h_rest[t][:], acc[:], 0.0)
+            else:
+                nc.scalar.activation(h_rest[t][:], acc[:], RELU)
         for t in (0, 2, 1, 3):
             scatter(t, rest, h_rest[t][:])
 
@@ -189,10 +192,10 @@ def tile_picked_devox_none_po_kernel(
         w2_scale = keep.tile([P, PACK, P], U8, name="w2_scale", align_bytes=64)
         nc.gpsimd.tensor_copy(w2_scale[:], w2_scale_raw[:].rearrange("p (m t) -> p t m", t=PACK))
 
-        gate_cols = keep.tile([P, D, V // P], F32, name="gate_cols")
+        gate_cols = keep.tile([P, 2, V // P], F32, name="gate_cols")
         turned = bank(4, P)
         turn(turned, gate_rows[:], True, True)
-        nc.vector.tensor_copy(gate_cols[:].rearrange("p d b -> p (d b)"), turned[:, 0 : D * V // P])
+        nc.vector.tensor_copy(gate_cols[:].rearrange("p d b -> p (d b)"), turned[:, 0 : 2 * V // P])
 
         quarter = [slice(c * QUARTER, (c + 1) * QUARTER) for c in range(4)]
         z_codes, z_scale = mx_tiles("z", U)
@@ -200,7 +203,7 @@ def tile_picked_devox_none_po_kernel(
         def turn_block(target, source, first, last):
             nc.tensor.matmul(target, source, identity[:], start=first, stop=last, is_transpose=True)
 
-        def turned_pairs(u, banks, copy):
+        def turned_pairs(u, banks, copies):
             turned = [bank(k) for k in banks]
             sources = [(tiles[2 * u + e], e) for tiles in (emb_t, windows) for e in range(2)]
             for i, (source, e) in enumerate(sources):
@@ -211,7 +214,7 @@ def tile_picked_devox_none_po_kernel(
                         turn_block(turned[c][:, place : place + P], source[:, cells], i + b == 0, i + b == len(sources))
             for c in range(2):
                 pairs[u, c] = keep.tile([P, 2, P, 2], BF16, name=f"z_pairs{u}_{c}", align_bytes=64)
-                copy(pairs[u, c][:], turned[c][:].rearrange("q (b e p) -> q b p e", b=2, e=2))
+                copies[c](pairs[u, c][:], turned[c][:].rearrange("q (b e p) -> q b p e", b=2, e=2))
 
         z_rows = {c: keep.tile([P, PACK, QUARTER], BF16, name=f"z_rows{c}", tag=f"z_rows{c - 2}", align_bytes=64) for c in (2, 3)}
 
@@ -223,11 +226,11 @@ def tile_picked_devox_none_po_kernel(
             for c in (2, 3):
                 add_emb(nc.gpsimd, t, c)
         pairs = {}
-        turned_pairs(0, (5, 6), nc.vector.tensor_copy)
+        turned_pairs(0, (5, 6), (nc.vector.tensor_copy, nc.scalar.copy))
         for t in (2, 3):
             for c in (2, 3):
                 add_emb(nc.vector, t, c)
-        turned_pairs(1, (0, 1), nc.scalar.copy)
+        turned_pairs(1, (0, 1), (nc.scalar.copy, nc.scalar.copy))
         z_grouped = [keep.tile([P, QUARTER, PACK], BF16, name=f"z_grouped{c}", align_bytes=64) for c in range(4)]
         for c in (2, 3):
             nc.vector.tensor_copy(
@@ -271,7 +274,7 @@ def tile_picked_devox_none_po_kernel(
 
         def later_y(t):
             for a in range(2):
-                acc = bank((4, 1 if t == 1 else 7)[a])
+                acc = bank((4, (1, 2, 7)[t - 1])[a])
                 second_layer(acc[:], t, slice(a * HALF, (a + 1) * HALF))
                 nc.scalar.copy(y_t[t][:, a * HALF : (a + 1) * HALF], acc[:])
 
@@ -295,7 +298,7 @@ def tile_picked_devox_none_po_kernel(
             weighted = keep.tile([P, V], F32, name=f"weighted{t}_{d}", tag=f"weighted{t}_{d}", align_bytes=64)
             for b in range(V // P):
                 block = slice(b * P, (b + 1) * P)
-                nc.scalar.activation(weighted[:, block], turned[:, block], COPY, scale=gate_cols[:, d, b : b + 1])
+                nc.scalar.activation(weighted[:, block], turned[:, block], COPY, scale=gate_cols[:, d - 1, b : b + 1])
             turn(back, weighted[:], d == 1, d == D - 1)
 
         def finish(t, back, term):

@@ -75,7 +75,7 @@ def tile_picked_devox_none_po_kernel(
 
         x_scale_table = keep.tile([P, T], U8, name="x_scale_table", align_bytes=64)
         nc.gpsimd.memset(x_scale_table[:].bitcast(I32), 0)
-        w2_scale_raw = keep.tile([P, H], U8, name="w2_scale_raw", tag="z_rows1", align_bytes=64)
+        w2_scale_raw = keep.tile([P, H], U8, name="w2_scale_raw", tag="z_rows", align_bytes=64)
         nc.gpsimd.memset(w2_scale_raw[:].bitcast(I32), 0)
         identity = keep.tile([P, P], F32, name="identity")
         make_identity(nc, identity[:])
@@ -99,7 +99,7 @@ def tile_picked_devox_none_po_kernel(
         cell_t = load_list("cell", cell)
         emb_rows = emb.rearrange("(p t) c -> p t c", t=PACK)
         emb_t = [keep.tile([P, U if t < 2 else HALF], F32, name=f"emb{t}") for t in range(PACK)]
-        w2_raw = keep.tile([P, 2 * H], U8, name="w2_raw", tag="z_rows0", align_bytes=64)
+        w2_raw = keep.tile([P, 2 * H], U8, name="w2_raw", align_bytes=64)
         nc.sync.dma_start(w2_raw[:].bitcast(I32), w2_words[0].bitcast(I32))
         load_scale_rows(w2_scale_raw, w2_scales)
         for t in (0, 2, 1, 3):
@@ -216,26 +216,21 @@ def tile_picked_devox_none_po_kernel(
                 pairs[u, c] = keep.tile([P, 2, P, 2], BF16, name=f"z_pairs{u}_{c}", align_bytes=64)
                 copies[c](pairs[u, c][:], turned[c][:].rearrange("q (b e p) -> q b p e", b=2, e=2))
 
-        z_rows = {c: keep.tile([P, PACK, QUARTER], BF16, name=f"z_rows{c}", tag=f"z_rows{c - 2}", align_bytes=64) for c in (2, 3)}
-
-        def add_emb(engine, t, c):
-            part = emb_t[t][:, quarter[c]] if t < 2 else emb_upper[:, t - 2, quarter[c - 2]]
-            engine.tensor_tensor(z_rows[c][:, t, :], windows[t][:, quarter[c]], part, ADD)
-
+        z_rows = keep.tile([P, PACK, HALF], BF16, name="z_rows", tag="z_rows", align_bytes=64)
         for t in range(2):
-            for c in (2, 3):
-                add_emb(nc.gpsimd, t, c)
+            nc.gpsimd.tensor_tensor(z_rows[:, t, :], windows[t][:, HALF:U], emb_t[t][:, HALF:U], ADD)
         pairs = {}
         turned_pairs(0, (5, 6), (nc.vector.tensor_copy, nc.scalar.copy))
         for t in (2, 3):
             for c in (2, 3):
-                add_emb(nc.vector, t, c)
+                cells = quarter[c - 2]
+                nc.vector.tensor_tensor(z_rows[:, t, cells], windows[t][:, quarter[c]], emb_upper[:, t - 2, cells], ADD)
         turned_pairs(1, (0, 1), (nc.scalar.copy, nc.scalar.copy))
         z_grouped = [keep.tile([P, QUARTER, PACK], BF16, name=f"z_grouped{c}", align_bytes=64) for c in range(4)]
         for c in (2, 3):
             nc.vector.tensor_copy(
                 z_grouped[c][:].rearrange("p (n i) t -> p n t i", i=4),
-                z_rows[c][:].rearrange("p t (n i) -> p n t i", i=4),
+                z_rows[:, :, quarter[c - 2]].rearrange("p t (n i) -> p n t i", i=4),
             )
         for c in range(2):
             back = bank(2 + c)
@@ -274,7 +269,7 @@ def tile_picked_devox_none_po_kernel(
 
         def later_y(t):
             for a in range(2):
-                acc = bank((4, (1, 2, 7)[t - 1])[a])
+                acc = bank((4, 1 if t == 1 else 7)[a])
                 second_layer(acc[:], t, slice(a * HALF, (a + 1) * HALF))
                 nc.scalar.copy(y_t[t][:, a * HALF : (a + 1) * HALF], acc[:])
 
@@ -294,12 +289,14 @@ def tile_picked_devox_none_po_kernel(
             turn(turned, plain[:], True, True)
             return turned
 
-        def gate_turned(back, turned, t, d):
+        def gate_turned(backs, turned, t, d):
             weighted = keep.tile([P, V], F32, name=f"weighted{t}_{d}", tag=f"weighted{t}_{d}", align_bytes=64)
             for b in range(V // P):
                 block = slice(b * P, (b + 1) * P)
                 nc.scalar.activation(weighted[:, block], turned[:, block], COPY, scale=gate_cols[:, d - 1, b : b + 1])
-            turn(back, weighted[:], d == 1, d == D - 1)
+            width = V // len(backs)
+            for a, back in enumerate(backs):
+                turn(back, weighted[:, a * width : (a + 1) * width], d == 1, d == D - 1)
 
         def finish(t, back, term):
             nc.vector.tensor_tensor(result[:, t, :], back[:], term[:], ADD)
@@ -307,30 +304,29 @@ def tile_picked_devox_none_po_kernel(
 
         whole = slice(0, V)
         later_y(1)
-        own0 = gated(0, 0, whole)
-        turned0 = [fetch_turned(0, 1)]
+        terms0 = [gated(0, d, whole) for d in range(D)]
         later_y(2)
-        turned0.append(fetch_turned(0, 2))
+        turned1 = [fetch_turned(1, d) for d in (1, 2)]
         later_y(3)
-        terms1 = [gated(1, d, whole) for d in range(D)]
+        own1 = gated(1, 0, whole)
         own2 = gated(2, 0, whole)
-        back0 = bank(5)
+        back1 = bank(5)
         for d in (1, 2):
-            gate_turned(back0, turned0[d - 1], 0, d)
-        turned1 = bank(2)
+            gate_turned([back1], turned1[d - 1], 1, d)
+        turned0 = bank(3)
         for d in range(D):
-            turn(turned1, terms1[d][:], d == 0, d == D - 1)
-        pair1 = keep.tile([P, V], F32, name="pair1")
-        nc.scalar.copy(pair1[:], turned1[:])
-        back1 = bank(6)
-        turn(back1, pair1[:], True, True)
+            turn(turned0, terms0[d][:], d == 0, d == D - 1)
+        sum0 = keep.tile([P, V], F32, name="sum0")
+        nc.scalar.copy(sum0[:], turned0[:])
+        back0 = bank(6)
+        turn(back0, sum0[:], True, True)
         terms3 = [gated(3, d, whole) for d in range(2)]
-        finish(0, back0, own0)
+        finish(1, back1, own1)
         turned2 = [fetch_turned(2, 1)]
-        nc.scalar.copy(result[:, 1, :], back1[:])
-        nc.sync.dma_start(out_rows[:, 1, :], result[:, 1, :])
+        nc.scalar.copy(result[:, 0, :], back0[:])
+        nc.sync.dma_start(out_rows[:, 0, :], result[:, 0, :])
         turned2.append(fetch_turned(2, 2))
-        back2 = bank(3)
+        back2 = [bank(k, V // 2) for k in (2, 4)]
         for d in (1, 2):
             gate_turned(back2, turned2[d - 1], 2, d)
         partial = keep.tile([P, V], F32, name="partial")
@@ -346,7 +342,7 @@ def tile_picked_devox_none_po_kernel(
         for a in range(2):
             place_pair(nc.scalar.copy, grouped[a], result[:, 0:2, halves[a]], 0)
         for a in range(2):
-            nc.vector.tensor_tensor(result[:, 2, halves[a]], back2[:, halves[a]], own2[:, halves[a]], ADD)
+            nc.vector.tensor_tensor(result[:, 2, halves[a]], back2[a][:], own2[:, halves[a]], ADD)
             nc.sync.dma_start(out_rows[:, 2, halves[a]], result[:, 2, halves[a]])
 
         codes, scale = mx_tiles("out", V)

from contextlib import ExitStack

import concourse.mybir as mybir
from concourse.masks import make_identity

FLOPS = 805306368

F32 = mybir.dt.float32
BF16 = mybir.dt.bfloat16
I32 = mybir.dt.int32
U32 = mybir.dt.uint32
U16 = mybir.dt.uint16
U8 = mybir.dt.uint8
FP8X4 = mybir.dt.float8_e4m3fn_x4
FP4X4 = mybir.dt.float4_e2m1fn_x4
ADD = mybir.AluOpType.add
MULT = mybir.AluOpType.mult
RELU = mybir.ActivationFunctionType.Relu
COPY = mybir.ActivationFunctionType.Copy

P = 128
PACK = 4
T, S, V, H, U, D = 2048, 512, 512, 512, 1024, 3
HALF = 512
QUARTER = 256


def tile_picked_devox_none_po_kernel(
    tc, x_words, x_scales, w1, w2_words, w2_scales, gate, emb, offs, cell, pos1, pos2, pos3, out_0, out_1, out_2
):
    nc = tc.nc
    with ExitStack() as ctx:
        lists = ctx.enter_context(tc.tile_pool(name="lists", bufs=1))
        keep = ctx.enter_context(tc.tile_pool(name="keep", bufs=1))
        psum = ctx.enter_context(tc.psum_pool(name="psum", bufs=1))

        def bank(k, columns=HALF):
            return psum.tile([P, columns], F32, name=f"bank{k}", tag=f"bank{k}")

        def load_list(name, src):
            tile = lists.tile([P, S // 16], U16, name=name)
            nc.sync.dma_start(tile[:], src)
            return tile

        def entries(tile, cols):
            return tile[:, cols.start // 16 : cols.stop // 16]

        def load_scale_rows(tile, rows):
            for q in range(4):
                nc.sync.dma_start(tile[32 * q : 32 * q + 4, :].bitcast(I32), rows[0, 4 * q : 4 * q + 4, :].bitcast(I32))

        def mx_tiles(name, width):
            codes = keep.tile([P, width], U32, name=f"{name}_codes", align_bytes=64)
            scale = keep.tile([P, width], U8, name=f"{name}_scale", align_bytes=64)
            return codes, scale

        def quantize_into(codes, scale, grouped):
            nc.vector.quantize_mx(out=codes.bitcast(FP8X4), scales=scale, in_=grouped)

        def turn(target, source, first, last):
            blocks = source.shape[1] // P
            for b in range(blocks):
                cols = slice(b * P, (b + 1) * P)
                nc.tensor.matmul(
                    target[:, cols],
                    source[:, cols],
                    identity[:],
                    start=(first and b == 0),
                    stop=(last and b == blocks - 1),
                    is_transpose=True,
                )

        def place_pair(copy, grouped, pair, u):
            copy(grouped[:, :, 2 * u : 2 * u + 2], pair.rearrange("p e c -> p c e"))

        x_scale_table = keep.tile([P, T], U8, name="x_scale_table", align_bytes=64)
        nc.gpsimd.memset(x_scale_table[:].bitcast(I32), 0)
        w2_scale_raw = keep.tile([P, H], U8, name="w2_scale_raw", tag="z_rows", align_bytes=64)
        nc.gpsimd.memset(w2_scale_raw[:].bitcast(I32), 0)
        identity = keep.tile([P, P], F32, name="identity")
        make_identity(nc, identity[:])

        w1_rows = w1.rearrange("(p j) c -> p j c", j=PACK)
        w1_raw = [keep.tile([P, PACK, H // 2], F32, name=f"w1_raw{h}") for h in range(2)]
        nc.sync.dma_start(w1_raw[0][:], w1_rows[:, :, 0 : H // 2])
        offs_t = load_list("offs", offs)
        nc.sync.dma_start(x_scale_table[0:P:8, :].bitcast(I32), x_scales[0].bitcast(I32))
        nc.sync.dma_start(w1_raw[1][:], w1_rows[:, :, H // 2 : H])
        x_word_table = keep.tile([P, T], U32, name="x_word_table", align_bytes=64)
        nc.sync.dma_start(x_word_table[:].bitcast(I32), x_words[0].rearrange("p n t -> p (n t)").bitcast(I32))
        x_scale_spread = keep.tile([P, S], U8, name="x_scale_spread", align_bytes=64)
        nc.vector.tensor_copy(x_scale_spread[:], x_scale_table[:].indirect(offs_t[:]))
        x_scale = keep.tile([P, S], U8, name="x_scale", align_bytes=64)
        nc.gpsimd.memset(x_scale[:].bitcast(I32), 0)
        for q in range(4):
            nc.sync.dma_start(
                x_scale[32 * q : 32 * q + 4, :].bitcast(I32), x_scale_spread[32 * q : 32 * q + 32 : 8, :].bitcast(I32)
            )
        cell_t = load_list("cell", cell)
        emb_rows = emb.rearrange("(p t) c -> p t c", t=PACK)
        emb_t = [keep.tile([P, U if t < 2 else HALF], F32, name=f"emb{t}") for t in range(PACK)]
        w2_raw = keep.tile([P, 2 * H], U8, name="w2_raw", align_bytes=64)
        nc.sync.dma_start(w2_raw[:].bitcast(I32), w2_words[0].bitcast(I32))
        load_scale_rows(w2_scale_raw, w2_scales)
        for t in (0, 2, 1, 3):
            nc.sync.dma_start(emb_t[t][:], emb_rows[:, t, 0 : emb_t[t].shape[1]])
        emb_upper = keep.tile([P, 2, HALF], F32, name="emb_upper")
        nc.sync.dma_start(emb_upper[:], emb_rows[:, 2:4, HALF:U])
        gate_rows = keep.tile([P, P], F32, name="gate_rows")
        nc.gpsimd.memset(gate_rows[:], 0.0)
        for d in (1, 2):
            nc.sync.dma_start(gate_rows[4 * d - 4 : 4 * d, :], gate[d, 0, :].rearrange("(b c) -> b c", c=P))
        pos_t = [load_list(f"pos{d + 1}", src) for d, src in enumerate((pos1, pos2, pos3))]
        gate_t = []
        for d in range(D):
            tile = keep.tile([P, V], F32, name=f"gate{d}")
            nc.sync.dma_start(tile[:], gate[d])
            gate_t.append(tile)

        windows = []
        for t in range(PACK):
            tile = keep.tile([P, U], F32, name=f"window{t}")
            (nc.vector if t < 2 else nc.gpsimd).memset(tile[:], 0.0)
            windows.append(tile)

        w1_grouped = keep.tile([P, PACK, P, PACK], BF16, name="w1_grouped", align_bytes=64)
        for h, copy in enumerate((nc.scalar.copy, nc.vector.tensor_copy)):
            rows = slice(h * (P // 2), (h + 1) * (P // 2))
            copy(
                w1_grouped[:, :, rows, :].rearrange("p t m j -> p m t j"),
                w1_raw[h][:].rearrange("p j (m t) -> p m t j", t=PACK),
            )
        w1_codes, w1_scale = mx_tiles("w1", H)
        quantize_into(w1_codes[:], w1_scale[:], w1_grouped[:].rearrange("p t m j -> p (t m j)"))

        head, rest = slice(0, P), slice(P, S)
        x_head = keep.tile([P, P], U32, name="x_head", align_bytes=64)
        nc.vector.tensor_copy(x_head[:], x_word_table[:].indirect(entries(offs_t, head)))
        x_rest = keep.tile([P, S - P], U32, name="x_rest", align_bytes=64)
        nc.vector.tensor_copy(x_rest[:], x_word_table[:].indirect(entries(offs_t, rest)))

        def x_codes(points):
            if points.start < P:
                return x_head[:, points]
            return x_rest[:, points.start - P : points.stop - P]

        def first_layer(acc, t, points):
            cols = slice(t * P, (t + 1) * P)
            nc.tensor.matmul_mx(
                out=acc,
                lhsT=w1_codes[:, cols].bitcast(FP8X4),
                lhsT_scale=w1_scale[:, cols],
                rhs=x_codes(points).bitcast(FP8X4),
                rhs_scale=x_scale[:, points],
                start=True,
                stop=True,
            )

        def scatter(t, points, values):
            target = windows[t][:].indirect(entries(cell_t, points))
            if t % 2 == 0:
                nc.vector.tensor_copy(target, values)
            else:
                nc.scalar.activation(target, values, COPY)

        h_head = []
        for u in range(2):
            acc = bank(u, 2 * P)
            for e in range(2):
                first_layer(acc[:, e * P : (e + 1) * P], 2 * u + e, head)
            h_head.append(keep.tile([P, 2, P], F32, name=f"h_head{u}"))
            nc.scalar.activation(h_head[u][:].rearrange("p e n -> p (e n)"), acc[:], RELU)
        for t in range(3):
            scatter(t, head, h_head[t // 2][:, t % 2, :])
        h_rest = {}
        for t, k in ((0, 2), (2, 3), (1, 4), (3, 7)):
            acc = bank(k, S - P)
            for points in (slice(P, 2 * P), slice(2 * P, S)):
                first_layer(acc[:, points.start - P : points.stop - P], t, points)
            if t == 3:
                scatter(3, head, h_head[1][:, 1, :])
            h_rest[t] = keep.tile([P, S - P], F32, name=f"h_rest{t}")
            if t == 2:
                nc.vector.tensor_scalar_max(h_rest[t][:], acc[:], 0.0)
            else:
                nc.scalar.activation(h_rest[t][:], acc[:], RELU)
        for t in (0, 2, 1, 3):
            scatter(t, rest, h_rest[t][:])

        w2_codes = keep.tile([P, PACK, P, 2], U8, name="w2_codes", align_bytes=64)
        nc.gpsimd.tensor_copy(w2_codes[:], w2_raw[:].rearrange("p (m t b) -> p t m b", t=PACK, b=2))
        w2_scale = keep.tile([P, PACK, P], U8, name="w2_scale", align_bytes=64)
        nc.gpsimd.tensor_copy(w2_scale[:], w2_scale_raw[:].rearrange("p (m t) -> p t m", t=PACK))

        gate_cols = keep.tile([P, 2, V // P], F32, name="gate_cols")
        turned = bank(4, P)
        turn(turned, gate_rows[:], True, True)
        nc.vector.tensor_copy(gate_cols[:].rearrange("p d b -> p (d b)"), turned[:, 0 : 2 * V // P])

        quarter = [slice(c * QUARTER, (c + 1) * QUARTER) for c in range(4)]
        z_codes, z_scale = mx_tiles("z", U)

        def turn_block(target, source, first, last):
            nc.tensor.matmul(target, source, identity[:], start=first, stop=last, is_transpose=True)

        def turned_pairs(u, banks, copies):
            turned = [bank(k) for k in banks]
            sources = [(tiles[2 * u + e], e) for tiles in (emb_t, windows) for e in range(2)]
            for i, (source, e) in enumerate(sources):
                for c in range(2):
                    for b in range(2):
                        cells = slice(c * QUARTER + b * P, c * QUARTER + (b + 1) * P)
                        place = (2 * b + e) * P
                        turn_block(turned[c][:, place : place + P], source[:, cells], i + b == 0, i + b == len(sources))
            for c in range(2):
                pairs[u, c] = keep.tile([P, 2, P, 2], BF16, name=f"z_pairs{u}_{c}", align_bytes=64)
                copies[c](pairs[u, c][:], turned[c][:].rearrange("q (b e p) -> q b p e", b=2, e=2))

        z_rows = keep.tile([P, PACK, HALF], BF16, name="z_rows", tag="z_rows", align_bytes=64)
        for t in range(2):
            nc.gpsimd.tensor_tensor(z_rows[:, t, :], windows[t][:, HALF:U], emb_t[t][:, HALF:U], ADD)
        pairs = {}
        turned_pairs(0, (5, 6), (nc.vector.tensor_copy, nc.scalar.copy))
        for t in (2, 3):
            for c in (2, 3):
                cells = quarter[c - 2]
                nc.vector.tensor_tensor(z_rows[:, t, cells], windows[t][:, quarter[c]], emb_upper[:, t - 2, cells], ADD)
        turned_pairs(1, (0, 1), (nc.scalar.copy, nc.scalar.copy))
        z_grouped = [keep.tile([P, QUARTER, PACK], BF16, name=f"z_grouped{c}", align_bytes=64) for c in range(4)]
        for c in (2, 3):
            nc.vector.tensor_copy(
                z_grouped[c][:].rearrange("p (n i) t -> p n t i", i=4),
                z_rows[:, :, quarter[c - 2]].rearrange("p t (n i) -> p n t i", i=4),
            )
        for c in range(2):
            back = bank(2 + c)
            for u in range(2):
                words = pairs[u, c][:].rearrange("q b p e -> q b (p e)").bitcast(F32)
                for b in range(2):
                    place = (2 * u + b) * P
                    nc.tensor.transpose(back[:, place : place + P], words[:, b, :], identity[:])
            for cells in ([slice(0, QUARTER)], [slice(0, P), slice(P, QUARTER)])[c]:
                nc.scalar.copy(
                    z_grouped[c][:, cells, :].rearrange("p n t -> p (n t)").bitcast(F32).rearrange("p (n u) -> p n u", u=2),
                    back[:].rearrange("p (u n) -> p n u", u=2)[:, cells, :],
                )
        parts = [(2, 0, QUARTER), (0, 0, QUARTER), (3, 0, QUARTER), (1, 0, P), (1, P, QUARTER)]
        z_cells = [slice(c * QUARTER + lo, c * QUARTER + hi) for c, lo, hi in parts]
        for (c, lo, hi), cells in zip(parts, z_cells):
            quantize_into(z_codes[:, cells], z_scale[:, cells], z_grouped[c][:, lo:hi, :].rearrange("p n t -> p (n t)"))

        def second_layer(acc, t, cells):
            nc.tensor.matmul_mx(
                out=acc,
                lhsT=w2_codes[:, t, :, :].rearrange("p m b -> p (m b)").bitcast(FP4X4),
                lhsT_scale=w2_scale[:, t, :],
                rhs=z_codes[:, cells].bitcast(FP8X4),
                rhs_scale=z_scale[:, cells],
                start=True,
                stop=True,
            )

        y_t = [keep.tile([P, U], F32, name=f"y{t}") for t in range(PACK)]
        for i, cells in enumerate(z_cells):
            acc = bank((4, 5, 7, 6, 0)[i], cells.stop - cells.start)
            second_layer(acc[:], 0, cells)
            copy = nc.vector.tensor_copy if i >= 3 else nc.scalar.copy
            copy(y_t[0][:, cells], acc[:])

        def later_y(t):
            for a in range(2):
                acc = bank((4, 1 if t == 1 else 7)[a])
                second_layer(acc[:], t, slice(a * HALF, (a + 1) * HALF))
                nc.scalar.copy(y_t[t][:, a * HALF : (a + 1) * HALF], acc[:])

        out_rows = out_0.rearrange("(p t) v -> p t v", t=PACK)
        result = keep.tile([P, PACK, V], F32, name="result")
        halves = [slice(a * (V // 2), (a + 1) * (V // 2)) for a in range(2)]

        def gated(t, d, cols):
            term = keep.tile([P, cols.stop - cols.start], F32, name=f"term{t}_{d}_{cols.start}")
            nc.vector.tensor_tensor(term[:], y_t[t][:].indirect(entries(pos_t[d], cols)), gate_t[d][:, cols], MULT)
            return term

        def fetch_turned(t, d):
            plain = keep.tile([P, V], F32, name=f"plain{t}_{d}", tag=f"plain{t}_{d}", align_bytes=64)
            nc.scalar.activation(plain[:], y_t[t][:].indirect(pos_t[d][:]), COPY)
            turned = bank(d - 1)
            turn(turned, plain[:], True, True)
            return turned

        def gate_turned(backs, turned, t, d):
            weighted = keep.tile([P, V], F32, name=f"weighted{t}_{d}", tag=f"weighted{t}_{d}", align_bytes=64)
            for b in range(V // P):
                block = slice(b * P, (b + 1) * P)
                nc.scalar.activation(weighted[:, block], turned[:, block], COPY, scale=gate_cols[:, d - 1, b : b + 1])
            width = V // len(backs)
            for a, back in enumerate(backs):
                turn(back, weighted[:, a * width : (a + 1) * width], d == 1, d == D - 1)

        def finish(t, back, term):
            nc.vector.tensor_tensor(result[:, t, :], back[:], term[:], ADD)
            nc.sync.dma_start(out_rows[:, t, :], result[:, t, :])

        whole = slice(0, V)
        later_y(1)
        terms0 = [gated(0, d, whole) for d in range(D)]
        later_y(2)
        turned1 = [fetch_turned(1, d) for d in (1, 2)]
        later_y(3)
        own1 = gated(1, 0, whole)
        own2 = gated(2, 0, whole)
        back1 = bank(5)
        for d in (1, 2):
            gate_turned([back1], turned1[d - 1], 1, d)
        turned0 = bank(3)
        for d in range(D):
            turn(turned0, terms0[d][:], d == 0, d == D - 1)
        sum0 = keep.tile([P, V], F32, name="sum0")
        nc.scalar.copy(sum0[:], turned0[:])
        back0 = bank(6)
        turn(back0, sum0[:], True, True)
        terms3 = [gated(3, d, whole) for d in range(2)]
        finish(1, back1, own1)
        turned2 = [fetch_turned(2, 1)]
        nc.scalar.copy(result[:, 0, :], back0[:])
        nc.sync.dma_start(out_rows[:, 0, :], result[:, 0, :])
        turned2.append(fetch_turned(2, 2))
        back2 = [bank(k, V // 2) for k in (2, 4)]
        for d in (1, 2):
            gate_turned(back2, turned2[d - 1], 2, d)
        partial = keep.tile([P, V], F32, name="partial")
        nc.vector.tensor_tensor(partial[:], terms3[0][:], terms3[1][:], ADD)
        late = [gated(3, 2, halves[a]) for a in range(2)]
        for a in range(2):
            nc.vector.tensor_tensor(result[:, 3, halves[a]], partial[:, halves[a]], late[a][:], ADD)
        nc.sync.dma_start(out_rows[:, 3, :], result[:, 3, :])
        grouped = [
            keep.tile([P, V // 2, PACK], BF16, name=f"out_grouped{a}", tag=tag, align_bytes=64)
            for a, tag in enumerate(("plain2_2", "weighted2_1"))
        ]
        for a in range(2):
            place_pair(nc.scalar.copy, grouped[a], result[:, 0:2, halves[a]], 0)
        for a in range(2):
            nc.vector.tensor_tensor(result[:, 2, halves[a]], back2[a][:], own2[:, halves[a]], ADD)
            nc.sync.dma_start(out_rows[:, 2, halves[a]], result[:, 2, halves[a]])

        codes, scale = mx_tiles("out", V)
        out_words = out_1[0].rearrange("p n t -> p (n t)").bitcast(I32)
        for a in range(2):
            place_pair(nc.vector.tensor_copy, grouped[a], result[:, 2:4, halves[a]], 1)
        for a in range(2):
            quantize_into(codes[:, halves[a]], scale[:, halves[a]], grouped[a][:].rearrange("p c t -> p (c t)"))
            nc.sync.dma_start(out_words[:, halves[a]], codes[:, halves[a]].bitcast(I32))
        for q in range(4):
            queue = nc.scalar if q % 2 == 0 else nc.sync
            queue.dma_start(out_2[0, 4 * q : 4 * q + 4, :].bitcast(I32), scale[32 * q : 32 * q + 4, :].bitcast(I32))
